import numpy as np
import ml_dtypes


def mxq(x, axis, fmt="e4m3"):
    dtype, down = {"e4m3": (ml_dtypes.float8_e4m3fn, 7), "e5m2": (ml_dtypes.float8_e5m2, 14)}[fmt]
    v = np.moveaxis(np.asarray(x, np.float32).astype(ml_dtypes.bfloat16).astype(np.float64), axis, -1)
    blocks = v.reshape(v.shape[:-1] + (-1, 32))
    amax = np.abs(blocks).max(-1, keepdims=True)
    byte = np.maximum(np.where(amax > 0, np.frexp(amax)[1] - 1 + 127, 0) - down, 1)
    scale = np.exp2(byte - 127.0)
    codes = (blocks / scale).astype(np.float32).astype(dtype).astype(np.float64)
    return np.moveaxis((codes * scale).reshape(v.shape), -1, axis)


WIDE = False


def mx_kscale(k):
    if not WIDE:
        return np.ones(k)
    levels = np.array([10, -10, 5, -5, 0])
    if k % 512:
        return np.exp2(np.random.permutation(np.resize(levels, k // 32))).repeat(32)
    a = np.empty((k // 512, 16))
    for p in range(k // 512):
        a[p, :8] = np.random.permutation(np.resize(levels, 8))
        for g in range(8):
            far = levels[np.abs(levels - a[p, g]) >= 10]
            a[p, g + 8] = far[np.random.randint(len(far))]
    return np.exp2(a.ravel()).repeat(32)


BF16 = ml_dtypes.bfloat16


def bf(x):
    return np.asarray(x, np.float32).astype(BF16)


def f64(x):
    return np.asarray(x).astype(np.float64)


B, N = 1536, 1024

STEP = 0.33
HEAT = 0.3


def setup_inputs():
    s = mx_kscale(N)
    q = np.random.standard_normal((B, N)) * s
    w = STEP * np.random.standard_normal((N, N)) / np.sqrt(N) / s[:, None] * s
    heater = HEAT * np.random.standard_normal(N) * s
    inv_cap = (1 + 0.1 * np.random.standard_normal(N)) / s
    return {"q": bf(q), "w": bf(w), "heater": bf(heater), "inv_cap": bf(inv_cap)}


def reference(q, w, heater, inv_cap):
    q0, h = f64(q), f64(heater)
    wq = mxq(f64(w), 0, "e4m3")
    d1 = mxq(q0, 1, "e4m3") @ wq
    q1 = q0 + d1 + h
    d2 = mxq(q1, 1, "e4m3") @ wq
    q2 = q1 + d2 + h
    d3 = mxq(q2, 1, "e4m3") @ wq
    q3 = q2 + d3
    return q3 * f64(inv_cap)

@@ -1,0 +1,345 @@
+from contextlib import ExitStack
+
+import concourse.mybir as mybir
+from concourse.masks import make_identity
+
+B, N = 1536, 1024
+FLOPS = 3 * 2 * B * N * N
+
+F32 = mybir.dt.float32
+BF16 = mybir.dt.bfloat16
+U32 = mybir.dt.uint32
+U8 = mybir.dt.uint8
+FP8X4 = mybir.dt.float8_e4m3fn_x4
+ADD = mybir.AluOpType.add
+MULT = mybir.AluOpType.mult
+COPY = mybir.ActivationFunctionType.Copy
+
+P = 128
+SIZES = [512, 512, 256, 256]
+NCH = len(SIZES)
+BASE = [sum(SIZES[:c]) for c in range(NCH)]
+LOADS = ['q0b', 'q0a', 'w00', 'w01', 'w11', 'q1a', 'w10', 'q1b', 'q2', 'q3']
+WENG = {'00': 'SV', '01': 'VS', '10': 'VS', '11': 'VS'}
+SCENG = {(0, 1): 'S', (2, 0): 'S', (3, 1): 'V', (3, 0): 'S', (1, 0): 'S', (2, 1): 'V', (0, 0): 'S'}
+ILENG = {(1, 3, 0): 'V'}
+OUTENG = {(2, 1): 'SSVV', (3, 0): 'SVVV', (2, 0): 'SSVS', (3, 1): 'SVSS', (1, 1): 'SSSS', (1, 0): 'SSSS'}
+FIRST = 0
+ORDER = [
+    "w 00 1",
+    "turn 0 1",
+    "turn 0 0",
+    "qq 0 0",
+    "w 00 0",
+    "w 01 0",
+    "w 01 1",
+    "wq 00",
+    "qq 0 1",
+    "w 11 0",
+    "w 11 1",
+    "w 10 0",
+    "w 10 1",
+    "turn 1 0",
+    "wq 01",
+    "wq 10",
+    "M1A004",
+    "turn 1 1",
+    "turn 2 0",
+    "il 1 0 0",
+    "qq 1 0",
+    "M1A104",
+    "il 1 0 1",
+    "M1B102",
+    "qq 2 0",
+    "M1B124",
+    "rq 1 0 1",
+    "il 1 1 1",
+    "M1B003",
+    "turn 3 0",
+    "M1B034",
+    "il 1 1 0",
+    "rq 1 0 0",
+    "M1C004",
+    "il 1 2 0",
+    "M2A004",
+    "il 2 0 0",
+    "qq 3 0",
+    "M2A104",
+    "il 2 0 1",
+    "sc 0 0",
+    "M1C104",
+    "il 1 2 1",
+    "sc 0 1",
+    "M1D004",
+    "rq 1 1 1",
+    "il 1 3 0",
+    "M1D102",
+    "rq 1 1 0",
+    "rq 2 0 0",
+    "M1D124",
+    "il 1 3 1",
+    "M2B002",
+    "rq 2 0 1",
+    "M2B024",
+    "il 2 1 0",
+    "M2B104",
+    "il 2 1 1",
+    "M3A002",
+    "rq 1 2 1",
+    "M3A023",
+    "rq 1 2 0",
+    "M3A034",
+    "rq 2 1 0",
+    "M3A103",
+    "rq 2 1 1",
+    "M3A134",
+    "out 0 0",
+    "sc 1 1",
+    "M2C002",
+    "sc 1 0",
+    "M2C024",
+    "il 2 2 0",
+    "M3B101",
+    "rq 1 3 0",
+    "M3B112",
+    "rq 1 3 1",
+    "out 0 1",
+    "M3B124",
+    "sc 2 0",
+    "M2C104",
+    "il 2 2 1",
+    "M2D002",
+    "rq 2 2 0",
+    "M2D024",
+    "il 2 3 0",
+    "M2D104",
+    "il 2 3 1",
+    "M3B001",
+    "rq 2 2 1",
+    "rq 2 3 0",
+    "M3B013",
+    "out 1 1",
+    "rq 2 3 1",
+    "sc 3 0",
+    "M3B034",
+    "M3C002",
+    "sc 2 1",
+    "M3C024",
+    "M3C104",
+    "sc 3 1",
+    "out 1 0",
+    "M3D004",
+    "out 2 0",
+    "out 2 1",
+    "M3D104",
+    "out 3 0",
+    "out 3 1",
+]
+
+
+def tile_dense_heat_steps_t1_kernel(tc, q, w, heater, inv_cap, out):
+    nc = tc.nc
+    with ExitStack() as ctx:
+        keep = ctx.enter_context(tc.tile_pool(name="keep", bufs=1))
+        stage = ctx.enter_context(tc.tile_pool(name="stage", bufs=3))
+        psum = ctx.enter_context(tc.psum_pool(name="psum", bufs=8))
+        ctx.enter_context(tc.manual_schedule())
+
+        ident = keep.tile([P, P], F32, name="ident")
+        warm = keep.tile([P, 1], F32, name="warm")
+        ivf = keep.tile([P, 2, 4], F32, name="ivf")
+        hv = keep.tile([P, 2, 4], BF16, name="hv")
+        iv = keep.tile([P, 2, 4], BF16, name="iv")
+        wraw = []
+        for h in range(2):
+            big = stage.tile([P, 2, 4, 512], BF16, name="big", align_bytes=256, bufs=8)
+            wraw.append(big)
+        wcodes = keep.tile([P, 2, 2, 512], U32, name="wcodes", align_bytes=256)
+        wscales = keep.tile([P, 2, 2, 512], U8, name="wscales", align_bytes=256)
+        qn = []
+        for c in range(NCH):
+            big = stage.tile([P, SIZES[c] // P, N], BF16, name="big", align_bytes=256, bufs=8)
+            qn.append(big)
+        qint = [keep.tile([P, 2, SIZES[c], 4], BF16, name="qint%d" % c, align_bytes=256) for c in range(NCH)]
+        state = [[keep.tile([P, 4, SIZES[c]], F32, name="state%d%d" % (c, g)) for g in range(2)] for c in range(NCH)]
+
+        def hbm_rows(x, c):
+            return x[BASE[c] : BASE[c] + SIZES[c], :].rearrange("(p b) k -> p b k", b=SIZES[c] // P)
+
+        make_identity(nc, ident[:])
+        nc.scalar.dma_start(out=hv[:], in_=heater.rearrange("(g p t) -> p g t", g=2, t=4))
+        for x in LOADS:
+            if x.startswith("w"):
+                h, g = int(x[1]), int(x[2])
+                src = w[512 * g : 512 * (g + 1), 512 * h : 512 * (h + 1)].rearrange("(p j) c -> p j c", j=4)
+                nc.sync.dma_start(out=wraw[h][:, g, :, :], in_=src)
+            else:
+                c, pr = int(x[1]), ("ab".index(x[2]) if len(x) > 2 else 0)
+                nc.sync.dma_start(out=qn[c][:, 2 * pr : 2 * pr + 2, :], in_=hbm_rows(q, c)[:, 2 * pr : 2 * pr + 2, :])
+        nc.vector.memset(warm[:], 0.0)
+        nc.scalar.activation(warm[:], warm[:], COPY, scale=1.0)
+        nc.gpsimd.dma_start(out=iv[:], in_=inv_cap.rearrange("(g p t) -> p g t", g=2, t=4))
+        nc.gpsimd.tensor_copy(out=ivf[:], in_=iv[:])
+
+        codes = {}
+        wgrp = {}
+        grp = {}
+
+        def get_codes(s, c):
+            if (s, c) not in codes:
+                cd = keep.tile([P, 2, SIZES[c]], U32, name="codes%d%d" % (s % 2, c), align_bytes=256)
+                sc = keep.tile([P, 2, SIZES[c]], U8, name="scales%d%d" % (s % 2, c), align_bytes=256)
+                codes[(s, c)] = (cd, sc)
+            return codes[(s, c)]
+
+        def do_wq(h, g):
+            if h == 0:
+                nc.vector.quantize_mx(out=wcodes[:, 0, g, :].bitcast(FP8X4), scales=wscales[:, 0, g, :], in_=wgrp[0][:, g, :])
+            else:
+                nc.vector.quantize_mx(
+                    out=wcodes[:, 1].rearrange("p g c -> p (g c)").bitcast(FP8X4),
+                    scales=wscales[:, 1].rearrange("p g c -> p (g c)"),
+                    in_=wgrp[1][:].rearrange("p g c -> p (g c)"),
+                )
+
+        def do_w(h, g, hf):
+            if h not in wgrp:
+                big = stage.tile([P, 2, 2048], BF16, name="big", align_bytes=256, bufs=8)
+                wgrp[h] = big
+            copy = nc.vector.tensor_copy if WENG["%d%d" % (h, g)][hf] == "V" else nc.scalar.copy
+            ts = slice(2 * hf, 2 * hf + 2)
+            copy(
+                out=wgrp[h][:, g, :].rearrange("p (t m j) -> p t m j", t=4, j=4)[:, ts],
+                in_=wraw[h][:, g, :, :].rearrange("p j (m t) -> p t m j", t=4)[:, ts],
+            )
+
+        def do_turn(c, pr):
+            for b in (2 * pr, 2 * pr + 1):
+                words = qn[c][:, b, :].bitcast(F32)
+                bank = psum.tile([P, 4, P], F32, name="bank")
+                for g in range(2):
+                    for u in range(2):
+                        nc.tensor.transpose(bank[:, 2 * g + u, :], words[:, 256 * g + u : 256 * (g + 1) : 2], ident[:])
+                dst = qint[c][:, :, P * b : P * (b + 1), :].rearrange("p g n t -> p g (n t)").bitcast(F32)
+                nc.scalar.copy(out=dst.rearrange("p g (n u) -> p g n u", u=2), in_=bank[:].rearrange("p (g u) n -> p g n u", g=2))
+
+        def do_qq(c, pr):
+            cd, sc = get_codes(1, c)
+            if c:
+                nc.vector.quantize_mx(
+                    out=cd[:].rearrange("p g n -> p (g n)").bitcast(FP8X4),
+                    scales=sc[:].rearrange("p g n -> p (g n)"),
+                    in_=qint[c][:].rearrange("p g n t -> p (g n t)"),
+                )
+                return
+            cols = slice(256 * pr, 256 * (pr + 1))
+            for g in range(2):
+                nc.vector.quantize_mx(out=cd[:, g, cols].bitcast(FP8X4), scales=sc[:, g, cols], in_=qint[c][:, g, cols, :].rearrange("p n t -> p (n t)"))
+
+        def one_pass(dst, s, c, go, t, g):
+            cd, sc = get_codes(s, c)
+            cols = slice(128 * t, 128 * (t + 1))
+            nc.tensor.matmul_mx(
+                out=dst,
+                lhsT=wcodes[:, go, g, cols].bitcast(FP8X4),
+                lhsT_scale=wscales[:, go, g, cols],
+                rhs=cd[:, g, :].bitcast(FP8X4),
+                rhs_scale=sc[:, g, :],
+                start=(g == 0),
+                stop=(g == 1),
+            )
+
+        first_banks = []
+
+        def do_mx(s, c, go, t0):
+            n = SIZES[c]
+            per = 512 // n
+            if (s, c, go) == (1, 0, FIRST) and n == 512:
+                if t0 == 0:
+                    for tt in range(4):
+                        bank = psum.tile([P, 512], F32, name="bank")
+                        first_banks.append(bank)
+                        one_pass(bank[:], s, c, go, tt, 0)
+                bank = first_banks[t0]
+                one_pass(bank[:], s, c, go, t0, 1)
+            else:
+                bank = psum.tile([P, 512], F32, name="bank")
+                for j in range(per):
+                    for g in range(2):
+                        one_pass(bank[:, n * j : n * (j + 1)], s, c, go, t0 + j, g)
+            for j in reversed(range(per)):
+                t = t0 + j
+                src = bank[:, n * j : n * (j + 1)]
+                st = state[c][go][:, t, :]
+                if s == 1:
+                    nc.vector.scalar_tensor_tensor(st, src, hv[:, go, t : t + 1], qint[c][:, go, :, t], ADD, ADD)
+                elif s == 2:
+                    nc.vector.scalar_tensor_tensor(st, src, hv[:, go, t : t + 1], st, ADD, ADD)
+                else:
+                    nc.vector.scalar_tensor_tensor(st, src, iv[:, go, t : t + 1], st, MULT, ADD)
+
+        def do_il(s, c, go):
+            grouped = stage.tile([P, SIZES[c], 4], BF16, name="grp", align_bytes=256, bufs=8)
+            for n0 in range(0, SIZES[c], 256):
+                n = slice(n0, n0 + 256)
+                copy = nc.vector.tensor_copy if ILENG.get((s, c, go)) == "V" else nc.scalar.copy
+                copy(
+                    out=grouped[:, n, :].rearrange("p (c i) t -> p c t i", i=4),
+                    in_=state[c][go][:, :, n].rearrange("p t (c i) -> p c t i", i=4),
+                )
+            grp[(s, c, go)] = grouped
+
+        def do_sc(c, go):
+            for t in range(4):
+                st = state[c][go][:, t, :]
+                if SCENG.get((c, go)) == "S":
+                    nc.scalar.activation(st, st, COPY, scale=ivf[:, go, t : t + 1])
+                else:
+                    nc.vector.tensor_scalar_mul(st, st, ivf[:, go, t : t + 1])
+
+        def do_rq(s, c, go):
+            cd, sc = get_codes(s + 1, c)
+            nc.vector.quantize_mx(out=cd[:, go, :].bitcast(FP8X4), scales=sc[:, go, :], in_=grp[(s, c, go)][:].rearrange("p n t -> p (n t)"))
+
+        count = {"out": 0}
+
+        def do_out(c, go):
+            count["out"] += 1
+            dst = hbm_rows(out, c)
+            nb = SIZES[c] // P
+            res = stage.tile([P, nb, 512], F32, name="big", align_bytes=256, bufs=8)
+            last = count["out"] == 2 * NCH
+            banks = []
+            if last:
+                for b in range(nb):
+                    bank = psum.tile([P, 4, P], F32, name="bank")
+                    banks.append(bank)
+                for t in range(4):
+                    for b in range(nb):
+                        nc.tensor.transpose(banks[b][:, t, :], state[c][go][:, t, P * b : P * (b + 1)], ident[:])
+            for b in range(nb):
+                if last:
+                    bank = banks[b]
+                else:
+                    bank = psum.tile([P, 4, P], F32, name="bank")
+                    for t in range(4):
+                        nc.tensor.transpose(bank[:, t, :], state[c][go][:, t, P * b : P * (b + 1)], ident[:])
+                copy = nc.vector.tensor_copy if OUTENG.get((c, go), "SVSV" if last else "SSSS")[b] == "V" else nc.scalar.copy
+                copy(out=res[:, b, :].rearrange("p (m t) -> p m t", t=4), in_=bank[:].rearrange("p t m -> p m t"))
+                nc.sync.dma_start(out=dst[:, b, 512 * go : 512 * (go + 1)], in_=res[:, b, :])
+
+        table = {"turn": do_turn, "qq": do_qq, "il": do_il, "rq": do_rq, "out": do_out, "sc": do_sc}
+        for line in ORDER:
+            if line.startswith("M"):
+                s, c, go = int(line[1]), "ABCD".index(line[2]), int(line[3])
+                first = int(line[4])
+                for t in range(first, int(line[5]), 512 // SIZES[c]):
+                    do_mx(s, c, go, t)
+            else:
+                parts = line.split(" ")
+                if parts[0] == "w":
+                    do_w(int(parts[1][0]), int(parts[1][1]), int(parts[2]))
+                elif parts[0] == "wq":
+                    do_wq(int(parts[1][0]), int(parts[1][1]))
+                else:
+                    table[parts[0]](*[int(v) for v in parts[1:]])

@@ -16,330 +16,219 @@ MULT = mybir.AluOpType.mult
 COPY = mybir.ActivationFunctionType.Copy
 
 P = 128
-SIZES = [512, 512, 256, 256]
-NCH = len(SIZES)
-BASE = [sum(SIZES[:c]) for c in range(NCH)]
-LOADS = ['q0b', 'q0a', 'w00', 'w01', 'w11', 'q1a', 'w10', 'q1b', 'q2', 'q3']
-WENG = {'00': 'SV', '01': 'VS', '10': 'VS', '11': 'VS'}
-SCENG = {(0, 1): 'S', (2, 0): 'S', (3, 1): 'V', (3, 0): 'S', (1, 0): 'S', (2, 1): 'V', (0, 0): 'S'}
-ILENG = {(1, 3, 0): 'V'}
-OUTENG = {(2, 1): 'SSVV', (3, 0): 'SVVV', (2, 0): 'SSVS', (3, 1): 'SVSS', (1, 1): 'SSSS', (1, 0): 'SSSS'}
-FIRST = 0
-ORDER = [
-    "w 00 1",
-    "turn 0 1",
-    "turn 0 0",
-    "qq 0 0",
-    "w 00 0",
-    "w 01 0",
-    "w 01 1",
-    "wq 00",
-    "qq 0 1",
-    "w 11 0",
-    "w 11 1",
-    "w 10 0",
-    "w 10 1",
-    "turn 1 0",
-    "wq 01",
-    "wq 10",
-    "M1A004",
-    "turn 1 1",
-    "turn 2 0",
-    "il 1 0 0",
-    "qq 1 0",
-    "M1A104",
-    "il 1 0 1",
-    "M1B102",
-    "qq 2 0",
-    "M1B124",
-    "rq 1 0 1",
-    "il 1 1 1",
-    "M1B003",
-    "turn 3 0",
-    "M1B034",
-    "il 1 1 0",
-    "rq 1 0 0",
-    "M1C004",
-    "il 1 2 0",
-    "M2A004",
-    "il 2 0 0",
-    "qq 3 0",
-    "M2A104",
-    "il 2 0 1",
-    "sc 0 0",
-    "M1C104",
-    "il 1 2 1",
-    "sc 0 1",
-    "M1D004",
-    "rq 1 1 1",
-    "il 1 3 0",
-    "M1D102",
-    "rq 1 1 0",
-    "rq 2 0 0",
-    "M1D124",
-    "il 1 3 1",
-    "M2B002",
-    "rq 2 0 1",
-    "M2B024",
-    "il 2 1 0",
-    "M2B104",
-    "il 2 1 1",
-    "M3A002",
-    "rq 1 2 1",
-    "M3A023",
-    "rq 1 2 0",
-    "M3A034",
-    "rq 2 1 0",
-    "M3A103",
-    "rq 2 1 1",
-    "M3A134",
-    "out 0 0",
-    "sc 1 1",
-    "M2C002",
-    "sc 1 0",
-    "M2C024",
-    "il 2 2 0",
-    "M3B101",
-    "rq 1 3 0",
-    "M3B112",
-    "rq 1 3 1",
-    "out 0 1",
-    "M3B124",
-    "sc 2 0",
-    "M2C104",
-    "il 2 2 1",
-    "M2D002",
-    "rq 2 2 0",
-    "M2D024",
-    "il 2 3 0",
-    "M2D104",
-    "il 2 3 1",
-    "M3B001",
-    "rq 2 2 1",
-    "rq 2 3 0",
-    "M3B013",
-    "out 1 1",
-    "rq 2 3 1",
-    "sc 3 0",
-    "M3B034",
-    "M3C002",
-    "sc 2 1",
-    "M3C024",
-    "M3C104",
-    "sc 3 1",
-    "out 1 0",
-    "M3D004",
-    "out 2 0",
-    "out 2 1",
-    "M3D104",
-    "out 3 0",
-    "out 3 1",
-]
+PAIR = 256
+SIZES = [256, 256, 256, 256, 256, 256]
+CHUNKS = len(SIZES)
+BASE = [sum(SIZES[:c]) for c in range(CHUNKS)]
+LAG = 2
 
 
 def tile_dense_heat_steps_t1_kernel(tc, q, w, heater, inv_cap, out):
     nc = tc.nc
     with ExitStack() as ctx:
         keep = ctx.enter_context(tc.tile_pool(name="keep", bufs=1))
-        stage = ctx.enter_context(tc.tile_pool(name="stage", bufs=3))
+        stage = ctx.enter_context(tc.tile_pool(name="stage", bufs=4))
         psum = ctx.enter_context(tc.psum_pool(name="psum", bufs=8))
         ctx.enter_context(tc.manual_schedule())
 
         ident = keep.tile([P, P], F32, name="ident")
         warm = keep.tile([P, 1], F32, name="warm")
-        ivf = keep.tile([P, 2, 4], F32, name="ivf")
-        hv = keep.tile([P, 2, 4], BF16, name="hv")
-        iv = keep.tile([P, 2, 4], BF16, name="iv")
-        wraw = []
-        for h in range(2):
-            big = stage.tile([P, 2, 4, 512], BF16, name="big", align_bytes=256, bufs=8)
-            wraw.append(big)
-        wcodes = keep.tile([P, 2, 2, 512], U32, name="wcodes", align_bytes=256)
-        wscales = keep.tile([P, 2, 2, 512], U8, name="wscales", align_bytes=256)
-        qn = []
-        for c in range(NCH):
-            big = stage.tile([P, SIZES[c] // P, N], BF16, name="big", align_bytes=256, bufs=8)
-            qn.append(big)
-        qint = [keep.tile([P, 2, SIZES[c], 4], BF16, name="qint%d" % c, align_bytes=256) for c in range(NCH)]
-        state = [[keep.tile([P, 4, SIZES[c]], F32, name="state%d%d" % (c, g)) for g in range(2)] for c in range(NCH)]
+        heat = keep.tile([P, 2, 4], BF16, name="heat")
+        inv16 = keep.tile([P, 2, 4], BF16, name="inv16")
+        inv = keep.tile([P, 2, 4], F32, name="inv")
+        w_codes = keep.tile([P, 2, 2, 512], U32, name="w_codes", align_bytes=256)
+        w_scales = keep.tile([P, 2, 2, 512], U8, name="w_scales", align_bytes=256)
+        q_words = [keep.tile([P, 2, SIZES[c], 4], BF16, name="q_words%d" % c, align_bytes=256) for c in range(CHUNKS)]
+        state = [[keep.tile([P, 4, SIZES[c]], F32, name="state%d%d" % (c, h)) for h in range(2)] for c in range(CHUNKS)]
 
         def hbm_rows(x, c):
             return x[BASE[c] : BASE[c] + SIZES[c], :].rearrange("(p b) k -> p b k", b=SIZES[c] // P)
 
+        q_rows = {}
+        w_rows = {}
+
+        def load_q(c, pair):
+            rows = keep.tile([P, 2, N], BF16, name="q_rows%d%d" % (c, pair), align_bytes=256)
+            nc.sync.dma_start(out=rows[:], in_=hbm_rows(q, c)[:, 2 * pair : 2 * pair + 2, :])
+            q_rows[(c, pair)] = rows
+
+        def load_w(h, g):
+            rows = stage.tile([P, 4, 512], BF16, name="half", align_bytes=256, bufs=8)
+            src = w[512 * g : 512 * (g + 1), 512 * h : 512 * (h + 1)].rearrange("(p j) c -> p j c", j=4)
+            nc.sync.dma_start(out=rows[:], in_=src)
+            w_rows[(h, g)] = rows
+
         make_identity(nc, ident[:])
-        nc.scalar.dma_start(out=hv[:], in_=heater.rearrange("(g p t) -> p g t", g=2, t=4))
-        for x in LOADS:
-            if x.startswith("w"):
-                h, g = int(x[1]), int(x[2])
-                src = w[512 * g : 512 * (g + 1), 512 * h : 512 * (h + 1)].rearrange("(p j) c -> p j c", j=4)
-                nc.sync.dma_start(out=wraw[h][:, g, :, :], in_=src)
-            else:
-                c, pr = int(x[1]), ("ab".index(x[2]) if len(x) > 2 else 0)
-                nc.sync.dma_start(out=qn[c][:, 2 * pr : 2 * pr + 2, :], in_=hbm_rows(q, c)[:, 2 * pr : 2 * pr + 2, :])
+        nc.scalar.dma_start(out=heat[:], in_=heater.rearrange("(g p t) -> p g t", g=2, t=4))
+        load_q(0, 0)
+        load_w(0, 0)
+        load_w(0, 1)
+        load_q(1, 0)
+        load_w(1, 0)
+        load_w(1, 1)
+        load_q(2, 0)
+        load_q(3, 0)
+        load_q(4, 0)
+        load_q(5, 0)
+        nc.sync.dma_start(out=inv16[:], in_=inv_cap.rearrange("(g p t) -> p g t", g=2, t=4))
         nc.vector.memset(warm[:], 0.0)
         nc.scalar.activation(warm[:], warm[:], COPY, scale=1.0)
-        nc.gpsimd.dma_start(out=iv[:], in_=inv_cap.rearrange("(g p t) -> p g t", g=2, t=4))
-        nc.gpsimd.tensor_copy(out=ivf[:], in_=iv[:])
 
         codes = {}
-        wgrp = {}
-        grp = {}
+        grouped = {}
+        w_grouped = {}
 
-        def get_codes(s, c):
+        def codes_of(s, c):
             if (s, c) not in codes:
                 cd = keep.tile([P, 2, SIZES[c]], U32, name="codes%d%d" % (s % 2, c), align_bytes=256)
                 sc = keep.tile([P, 2, SIZES[c]], U8, name="scales%d%d" % (s % 2, c), align_bytes=256)
                 codes[(s, c)] = (cd, sc)
             return codes[(s, c)]
 
-        def do_wq(h, g):
-            if h == 0:
-                nc.vector.quantize_mx(out=wcodes[:, 0, g, :].bitcast(FP8X4), scales=wscales[:, 0, g, :], in_=wgrp[0][:, g, :])
-            else:
-                nc.vector.quantize_mx(
-                    out=wcodes[:, 1].rearrange("p g c -> p (g c)").bitcast(FP8X4),
-                    scales=wscales[:, 1].rearrange("p g c -> p (g c)"),
-                    in_=wgrp[1][:].rearrange("p g c -> p (g c)"),
-                )
-
-        def do_w(h, g, hf):
-            if h not in wgrp:
-                big = stage.tile([P, 2, 2048], BF16, name="big", align_bytes=256, bufs=8)
-                wgrp[h] = big
-            copy = nc.vector.tensor_copy if WENG["%d%d" % (h, g)][hf] == "V" else nc.scalar.copy
-            ts = slice(2 * hf, 2 * hf + 2)
+        def group_w(h, g, copy, ts=slice(0, 4)):
+            if (h, g) not in w_grouped:
+                dst = stage.tile([P, 2048], BF16, name="half", align_bytes=256, bufs=8)
+                w_grouped[(h, g)] = dst
             copy(
-                out=wgrp[h][:, g, :].rearrange("p (t m j) -> p t m j", t=4, j=4)[:, ts],
-                in_=wraw[h][:, g, :, :].rearrange("p j (m t) -> p t m j", t=4)[:, ts],
+                out=w_grouped[(h, g)][:].rearrange("p (t m j) -> p t m j", t=4, j=4)[:, ts],
+                in_=w_rows[(h, g)][:].rearrange("p j (m t) -> p t m j", t=4)[:, ts],
             )
 
-        def do_turn(c, pr):
-            for b in (2 * pr, 2 * pr + 1):
-                words = qn[c][:, b, :].bitcast(F32)
+        def quantize_w(h, g):
+            nc.vector.quantize_mx(out=w_codes[:, h, g, :].bitcast(FP8X4), scales=w_scales[:, h, g, :], in_=w_grouped[(h, g)][:])
+
+        def turn_q(c, pair):
+            for b in (2 * pair, 2 * pair + 1):
+                words = q_rows[(c, pair)][:, b % 2, :].bitcast(F32)
                 bank = psum.tile([P, 4, P], F32, name="bank")
                 for g in range(2):
                     for u in range(2):
                         nc.tensor.transpose(bank[:, 2 * g + u, :], words[:, 256 * g + u : 256 * (g + 1) : 2], ident[:])
-                dst = qint[c][:, :, P * b : P * (b + 1), :].rearrange("p g n t -> p g (n t)").bitcast(F32)
+                dst = q_words[c][:, :, P * b : P * (b + 1), :].rearrange("p g n t -> p g (n t)").bitcast(F32)
                 nc.scalar.copy(out=dst.rearrange("p g (n u) -> p g n u", u=2), in_=bank[:].rearrange("p (g u) n -> p g n u", g=2))
 
-        def do_qq(c, pr):
-            cd, sc = get_codes(1, c)
-            if c:
-                nc.vector.quantize_mx(
-                    out=cd[:].rearrange("p g n -> p (g n)").bitcast(FP8X4),
-                    scales=sc[:].rearrange("p g n -> p (g n)"),
-                    in_=qint[c][:].rearrange("p g n t -> p (g n t)"),
-                )
-                return
-            cols = slice(256 * pr, 256 * (pr + 1))
-            for g in range(2):
-                nc.vector.quantize_mx(out=cd[:, g, cols].bitcast(FP8X4), scales=sc[:, g, cols], in_=qint[c][:, g, cols, :].rearrange("p n t -> p (n t)"))
+        def quantize_q(c):
+            cd, sc = codes_of(0, c)
+            nc.vector.quantize_mx(
+                out=cd[:].rearrange("p g n -> p (g n)").bitcast(FP8X4),
+                scales=sc[:].rearrange("p g n -> p (g n)"),
+                in_=q_words[c][:].rearrange("p g n t -> p (g n t)"),
+            )
 
-        def one_pass(dst, s, c, go, t, g):
-            cd, sc = get_codes(s, c)
-            cols = slice(128 * t, 128 * (t + 1))
+        def one_pass(dst, s, c, h, t, g):
+            cd, sc = codes_of(s, c)
+            cells = slice(P * t, P * (t + 1))
             nc.tensor.matmul_mx(
                 out=dst,
-                lhsT=wcodes[:, go, g, cols].bitcast(FP8X4),
-                lhsT_scale=wscales[:, go, g, cols],
+                lhsT=w_codes[:, h, g, cells].bitcast(FP8X4),
+                lhsT_scale=w_scales[:, h, g, cells],
                 rhs=cd[:, g, :].bitcast(FP8X4),
                 rhs_scale=sc[:, g, :],
                 start=(g == 0),
                 stop=(g == 1),
             )
 
-        first_banks = []
-
-        def do_mx(s, c, go, t0):
+        def multiply(s, c, h, ts):
             n = SIZES[c]
-            per = 512 // n
-            if (s, c, go) == (1, 0, FIRST) and n == 512:
-                if t0 == 0:
-                    for tt in range(4):
-                        bank = psum.tile([P, 512], F32, name="bank")
-                        first_banks.append(bank)
-                        one_pass(bank[:], s, c, go, tt, 0)
-                bank = first_banks[t0]
-                one_pass(bank[:], s, c, go, t0, 1)
+            bank = psum.tile([P, 512], F32, name="bank")
+            for j, t in enumerate(ts):
+                for g in range(2):
+                    one_pass(bank[:, n * j : n * (j + 1)], s, c, h, t, g)
+            for j, t in enumerate(ts):
+                advance(bank[:, n * j : n * (j + 1)], s, c, h, t)
+
+        def advance(sums, s, c, h, t):
+            now = state[c][h][:, t, :]
+            if s == 0:
+                nc.vector.scalar_tensor_tensor(now, sums, heat[:, h, t : t + 1], q_words[c][:, h, :, t], ADD, ADD)
+            elif s == 1:
+                nc.vector.scalar_tensor_tensor(now, sums, heat[:, h, t : t + 1], now, ADD, ADD)
+            elif c == CHUNKS - 1:
+                nc.vector.scalar_tensor_tensor(now, sums, inv[:, h, t : t + 1], now, MULT, ADD)
             else:
-                bank = psum.tile([P, 512], F32, name="bank")
-                for j in range(per):
-                    for g in range(2):
-                        one_pass(bank[:, n * j : n * (j + 1)], s, c, go, t0 + j, g)
-            for j in reversed(range(per)):
-                t = t0 + j
-                src = bank[:, n * j : n * (j + 1)]
-                st = state[c][go][:, t, :]
-                if s == 1:
-                    nc.vector.scalar_tensor_tensor(st, src, hv[:, go, t : t + 1], qint[c][:, go, :, t], ADD, ADD)
-                elif s == 2:
-                    nc.vector.scalar_tensor_tensor(st, src, hv[:, go, t : t + 1], st, ADD, ADD)
-                else:
-                    nc.vector.scalar_tensor_tensor(st, src, iv[:, go, t : t + 1], st, MULT, ADD)
+                nc.vector.tensor_tensor(now, sums, now, ADD)
+                scale(c, h, t)
 
-        def do_il(s, c, go):
-            grouped = stage.tile([P, SIZES[c], 4], BF16, name="grp", align_bytes=256, bufs=8)
-            for n0 in range(0, SIZES[c], 256):
-                n = slice(n0, n0 + 256)
-                copy = nc.vector.tensor_copy if ILENG.get((s, c, go)) == "V" else nc.scalar.copy
-                copy(
-                    out=grouped[:, n, :].rearrange("p (c i) t -> p c t i", i=4),
-                    in_=state[c][go][:, :, n].rearrange("p t (c i) -> p c t i", i=4),
-                )
-            grp[(s, c, go)] = grouped
+        def scale(c, h, t):
+            now = state[c][h][:, t, :]
+            nc.gpsimd.tensor_scalar(now, now, inv[:, h, t : t + 1], 0.0, MULT, ADD)
 
-        def do_sc(c, go):
+        def prescale(c, h):
             for t in range(4):
-                st = state[c][go][:, t, :]
-                if SCENG.get((c, go)) == "S":
-                    nc.scalar.activation(st, st, COPY, scale=ivf[:, go, t : t + 1])
-                else:
-                    nc.vector.tensor_scalar_mul(st, st, ivf[:, go, t : t + 1])
+                now = state[c][h][:, t, :]
+                nc.vector.tensor_scalar_mul(now, now, inv[:, h, t : t + 1])
 
-        def do_rq(s, c, go):
-            cd, sc = get_codes(s + 1, c)
-            nc.vector.quantize_mx(out=cd[:, go, :].bitcast(FP8X4), scales=sc[:, go, :], in_=grp[(s, c, go)][:].rearrange("p n t -> p (n t)"))
+        def group_state(s, c, h):
+            dst = stage.tile([P, SIZES[c], 4], BF16, name="half", align_bytes=256, bufs=8)
+            nc.scalar.copy(
+                out=dst[:].rearrange("p (c i) t -> p c t i", i=4),
+                in_=state[c][h][:].rearrange("p t (c i) -> p c t i", i=4),
+            )
+            grouped[(s, c, h)] = dst
 
-        count = {"out": 0}
+        def quantize_state(s, c, h):
+            cd, sc = codes_of(s + 1, c)
+            src = grouped[(s, c, h)]
+            nc.vector.quantize_mx(out=cd[:, h, :].bitcast(FP8X4), scales=sc[:, h, :], in_=src[:].rearrange("p n t -> p (n t)"))
 
-        def do_out(c, go):
-            count["out"] += 1
-            dst = hbm_rows(out, c)
-            nb = SIZES[c] // P
-            res = stage.tile([P, nb, 512], F32, name="big", align_bytes=256, bufs=8)
-            last = count["out"] == 2 * NCH
-            banks = []
-            if last:
-                for b in range(nb):
-                    bank = psum.tile([P, 4, P], F32, name="bank")
-                    banks.append(bank)
+        def store(c, h, pair, share=False):
+            for b in (2 * pair, 2 * pair + 1):
+                bank = psum.tile([P, 4, P], F32, name="bank")
                 for t in range(4):
-                    for b in range(nb):
-                        nc.tensor.transpose(banks[b][:, t, :], state[c][go][:, t, P * b : P * (b + 1)], ident[:])
-            for b in range(nb):
-                if last:
-                    bank = banks[b]
-                else:
-                    bank = psum.tile([P, 4, P], F32, name="bank")
-                    for t in range(4):
-                        nc.tensor.transpose(bank[:, t, :], state[c][go][:, t, P * b : P * (b + 1)], ident[:])
-                copy = nc.vector.tensor_copy if OUTENG.get((c, go), "SVSV" if last else "SSSS")[b] == "V" else nc.scalar.copy
-                copy(out=res[:, b, :].rearrange("p (m t) -> p m t", t=4), in_=bank[:].rearrange("p t m -> p m t"))
-                nc.sync.dma_start(out=dst[:, b, 512 * go : 512 * (go + 1)], in_=res[:, b, :])
+                    nc.tensor.transpose(bank[:, t, :], state[c][h][:, t, P * b : P * (b + 1)], ident[:])
+                res = stage.tile([P, 512], F32, name="res", bufs=8)
+                copy = nc.vector.tensor_copy if share and b % 2 else nc.scalar.copy
+                copy(out=res[:].rearrange("p (m t) -> p m t", t=4), in_=bank[:].rearrange("p t m -> p m t"))
+                nc.sync.dma_start(out=hbm_rows(out, c)[:, b, 512 * h : 512 * (h + 1)], in_=res[:])
 
-        table = {"turn": do_turn, "qq": do_qq, "il": do_il, "rq": do_rq, "out": do_out, "sc": do_sc}
-        for line in ORDER:
-            if line.startswith("M"):
-                s, c, go = int(line[1]), "ABCD".index(line[2]), int(line[3])
-                first = int(line[4])
-                for t in range(first, int(line[5]), 512 // SIZES[c]):
-                    do_mx(s, c, go, t)
+        units = [(0, 0, 0), (0, 1, 0), (0, 0, 1), (0, 1, 1)]
+        for period in range(2, CHUNKS + 3):
+            for s, c in ((0, period), (1, period - 2), (2, period - 3)):
+                if 0 <= c < CHUNKS:
+                    units.extend([(s, c, 0), (s, c, 1)])
+
+        turn_q(0, 0)
+        group_w(0, 0, nc.vector.tensor_copy)
+        quantize_q(0)
+        quantize_w(0, 0)
+        group_w(0, 1, nc.scalar.copy, slice(2, 4))
+        group_w(0, 1, nc.vector.tensor_copy, slice(0, 2))
+        turn_q(1, 0)
+        quantize_w(0, 1)
+        group_w(1, 0, nc.vector.tensor_copy)
+        quantize_q(1)
+        group_w(1, 1, nc.scalar.copy)
+        nc.gpsimd.tensor_copy(out=inv[:], in_=inv16[:])
+        to_quantize = []
+        to_store = []
+        for i, (s, c, h) in enumerate(units):
+            for half in range(2):
+                multiply(s, c, h, (2 * half, 2 * half + 1))
+                quiet = s < 2 and (half == 1 or i == 0 or units[i - 1][0] < 2)
+                if to_quantize and to_quantize[0][0] <= i - 2 and (quiet or i >= len(units) - 4):
+                    unit = to_quantize.pop(0)[1:]
+                    quantize_state(*unit)
+                    if unit[:2] == (1, CHUNKS - 1):
+                        prescale(*unit[1:])
+            if i == 0:
+                quantize_w(1, 0)
+                quantize_w(1, 1)
+            if s == 0 and h == 1 and 1 <= c < CHUNKS - 2:
+                turn_q(c + 2, 0)
+            if i == 1:
+                turn_q(2, 0)
+            if i == 2:
+                quantize_q(2)
+            if s == 0 and h == 1 and 2 <= c < CHUNKS - 1:
+                quantize_q(c + 1)
+            if to_store and to_store[0][0] <= i - LAG:
+                store(*to_store.pop(0)[1:])
+            if i == len(units) - 2:
+                store(*to_store.pop(0)[1:])
+            if s < 2:
+                group_state(s, c, h)
+                to_quantize.append((i, s, c, h))
             else:
-                parts = line.split(" ")
-                if parts[0] == "w":
-                    do_w(int(parts[1][0]), int(parts[1][1]), int(parts[2]))
-                elif parts[0] == "wq":
-                    do_wq(int(parts[1][0]), int(parts[1][1]))
-                else:
-                    table[parts[0]](*[int(v) for v in parts[1:]])
+                to_store.append((i, c, h, 0))
+        for job in to_store:
+            store(*job[1:], True)

@@ -16,11 +16,16 @@ MULT = mybir.AluOpType.mult
 COPY = mybir.ActivationFunctionType.Copy
 
 P = 128
-PAIR = 256
-SIZES = [256, 256, 256, 256, 256, 256]
-CHUNKS = len(SIZES)
-BASE = [sum(SIZES[:c]) for c in range(CHUNKS)]
-LAG = 2
+CHUNK = 512
+CHUNKS = B // CHUNK
+WHOLE = slice(0, CHUNK)
+PAIRS = [slice(0, 256), slice(256, 512)]
+LAST = CHUNKS - 1
+TQC = (1, 3)
+QDEF = (0,)
+QQC = [(7, 3), (8, 0)]
+QSLOT = {8: (), 9: (), 10: (3,), 11: (1,), 12: (0,), 13: (0,)}
+TSLOT = {10: (3,), 11: (3,), 12: (1, 3), 14: (3,), 16: (3,), 17: (3,), 18: (3,), 19: (3,), 20: (3,), 21: (3,)}
 
 
 def tile_dense_heat_steps_t1_kernel(tc, q, w, heater, inv_cap, out):
@@ -38,11 +43,12 @@ def tile_dense_heat_steps_t1_kernel(tc, q, w, heater, inv_cap, out):
         inv = keep.tile([P, 2, 4], F32, name="inv")
         w_codes = keep.tile([P, 2, 2, 512], U32, name="w_codes", align_bytes=256)
         w_scales = keep.tile([P, 2, 2, 512], U8, name="w_scales", align_bytes=256)
-        q_words = [keep.tile([P, 2, SIZES[c], 4], BF16, name="q_words%d" % c, align_bytes=256) for c in range(CHUNKS)]
-        state = [[keep.tile([P, 4, SIZES[c]], F32, name="state%d%d" % (c, h)) for h in range(2)] for c in range(CHUNKS)]
+        q_words = [keep.tile([P, 2, CHUNK, 4], BF16, name="q_words%d" % c, align_bytes=256) for c in range(CHUNKS)]
+        state = [[keep.tile([P, 4, CHUNK], F32, name="state%d%d" % (c, h)) for h in range(2)] for c in range(CHUNKS)]
+        scaled = [keep.tile([P, 4, CHUNK], F32, name="scaled%d" % h) for h in range(2)]
 
         def hbm_rows(x, c):
-            return x[BASE[c] : BASE[c] + SIZES[c], :].rearrange("(p b) k -> p b k", b=SIZES[c] // P)
+            return x[CHUNK * c : CHUNK * (c + 1), :].rearrange("(p b) k -> p b k", b=4)
 
         q_rows = {}
         w_rows = {}
@@ -60,16 +66,16 @@ def tile_dense_heat_steps_t1_kernel(tc, q, w, heater, inv_cap, out):
 
         make_identity(nc, ident[:])
         nc.scalar.dma_start(out=heat[:], in_=heater.rearrange("(g p t) -> p g t", g=2, t=4))
-        load_q(0, 0)
         load_w(0, 0)
+        load_q(0, 0)
         load_w(0, 1)
-        load_q(1, 0)
+        load_q(0, 1)
         load_w(1, 0)
         load_w(1, 1)
+        load_q(1, 0)
+        load_q(1, 1)
         load_q(2, 0)
-        load_q(3, 0)
-        load_q(4, 0)
-        load_q(5, 0)
+        load_q(2, 1)
         nc.sync.dma_start(out=inv16[:], in_=inv_cap.rearrange("(g p t) -> p g t", g=2, t=4))
         nc.vector.memset(warm[:], 0.0)
         nc.scalar.activation(warm[:], warm[:], COPY, scale=1.0)
@@ -80,8 +86,8 @@ def tile_dense_heat_steps_t1_kernel(tc, q, w, heater, inv_cap, out):
 
         def codes_of(s, c):
             if (s, c) not in codes:
-                cd = keep.tile([P, 2, SIZES[c]], U32, name="codes%d%d" % (s % 2, c), align_bytes=256)
-                sc = keep.tile([P, 2, SIZES[c]], U8, name="scales%d%d" % (s % 2, c), align_bytes=256)
+                cd = keep.tile([P, 2, CHUNK], U32, name="codes%d%d" % (s % 2, c), align_bytes=256)
+                sc = keep.tile([P, 2, CHUNK], U8, name="scales%d%d" % (s % 2, c), align_bytes=256)
                 codes[(s, c)] = (cd, sc)
             return codes[(s, c)]
 
@@ -107,69 +113,59 @@ def tile_dense_heat_steps_t1_kernel(tc, q, w, heater, inv_cap, out):
                 dst = q_words[c][:, :, P * b : P * (b + 1), :].rearrange("p g n t -> p g (n t)").bitcast(F32)
                 nc.scalar.copy(out=dst.rearrange("p g (n u) -> p g n u", u=2), in_=bank[:].rearrange("p (g u) n -> p g n u", g=2))
 
-        def quantize_q(c):
+        def quantize_q(c, g, cols):
             cd, sc = codes_of(0, c)
-            nc.vector.quantize_mx(
-                out=cd[:].rearrange("p g n -> p (g n)").bitcast(FP8X4),
-                scales=sc[:].rearrange("p g n -> p (g n)"),
-                in_=q_words[c][:].rearrange("p g n t -> p (g n t)"),
-            )
+            nc.vector.quantize_mx(out=cd[:, g, cols].bitcast(FP8X4), scales=sc[:, g, cols], in_=q_words[c][:, g, cols, :].rearrange("p n t -> p (n t)"))
 
-        def one_pass(dst, s, c, h, t, g):
+        def one_pass(bank, s, c, h, t, g, cols):
             cd, sc = codes_of(s, c)
             cells = slice(P * t, P * (t + 1))
             nc.tensor.matmul_mx(
-                out=dst,
+                out=bank[:, cols],
                 lhsT=w_codes[:, h, g, cells].bitcast(FP8X4),
                 lhsT_scale=w_scales[:, h, g, cells],
-                rhs=cd[:, g, :].bitcast(FP8X4),
-                rhs_scale=sc[:, g, :],
+                rhs=cd[:, g, cols].bitcast(FP8X4),
+                rhs_scale=sc[:, g, cols],
                 start=(g == 0),
                 stop=(g == 1),
             )
 
-        def multiply(s, c, h, ts):
-            n = SIZES[c]
-            bank = psum.tile([P, 512], F32, name="bank")
-            for j, t in enumerate(ts):
-                for g in range(2):
-                    one_pass(bank[:, n * j : n * (j + 1)], s, c, h, t, g)
-            for j, t in enumerate(ts):
-                advance(bank[:, n * j : n * (j + 1)], s, c, h, t)
+        def multiply(s, c, h, t, cols=WHOLE):
+            bank = psum.tile([P, CHUNK], F32, name="bank")
+            for g in range(2):
+                one_pass(bank, s, c, h, t, g, cols)
+            advance(bank, s, c, h, t, cols)
 
-        def advance(sums, s, c, h, t):
-            now = state[c][h][:, t, :]
+        def advance(bank, s, c, h, t, cols):
+            now = state[c][h][:, t, cols]
             if s == 0:
-                nc.vector.scalar_tensor_tensor(now, sums, heat[:, h, t : t + 1], q_words[c][:, h, :, t], ADD, ADD)
+                nc.vector.scalar_tensor_tensor(now, bank[:, cols], heat[:, h, t : t + 1], q_words[c][:, h, cols, t], ADD, ADD)
             elif s == 1:
-                nc.vector.scalar_tensor_tensor(now, sums, heat[:, h, t : t + 1], now, ADD, ADD)
-            elif c == CHUNKS - 1:
-                nc.vector.scalar_tensor_tensor(now, sums, inv[:, h, t : t + 1], now, MULT, ADD)
+                nc.vector.scalar_tensor_tensor(now, bank[:, cols], heat[:, h, t : t + 1], now, ADD, ADD)
+                if c == LAST:
+                    nc.gpsimd.tensor_scalar(scaled[h][:, t, cols], now, inv[:, h, t : t + 1], 0.0, MULT, ADD)
+            elif c == LAST:
+                nc.vector.scalar_tensor_tensor(now, bank[:, cols], inv[:, h, t : t + 1], scaled[h][:, t, cols], MULT, ADD)
             else:
-                nc.vector.tensor_tensor(now, sums, now, ADD)
-                scale(c, h, t)
+                nc.vector.tensor_tensor(now, bank[:, cols], now, ADD)
+                scale(c, h, t, cols)
 
-        def scale(c, h, t):
-            now = state[c][h][:, t, :]
+        def scale(c, h, t, cols):
+            now = state[c][h][:, t, cols]
             nc.gpsimd.tensor_scalar(now, now, inv[:, h, t : t + 1], 0.0, MULT, ADD)
 
-        def prescale(c, h):
-            for t in range(4):
-                now = state[c][h][:, t, :]
-                nc.vector.tensor_scalar_mul(now, now, inv[:, h, t : t + 1])
-
-        def group_state(s, c, h):
-            dst = stage.tile([P, SIZES[c], 4], BF16, name="half", align_bytes=256, bufs=8)
+        def group_state(s, c, h, cols):
+            dst = stage.tile([P, cols.stop - cols.start, 4], BF16, name="half", align_bytes=256, bufs=8)
             nc.scalar.copy(
                 out=dst[:].rearrange("p (c i) t -> p c t i", i=4),
-                in_=state[c][h][:].rearrange("p t (c i) -> p c t i", i=4),
+                in_=state[c][h][:, :, cols].rearrange("p t (c i) -> p c t i", i=4),
             )
-            grouped[(s, c, h)] = dst
+            grouped[(s, c, h, cols.start)] = dst
 
-        def quantize_state(s, c, h):
+        def quantize_state(s, c, h, cols):
             cd, sc = codes_of(s + 1, c)
-            src = grouped[(s, c, h)]
-            nc.vector.quantize_mx(out=cd[:, h, :].bitcast(FP8X4), scales=sc[:, h, :], in_=src[:].rearrange("p n t -> p (n t)"))
+            src = grouped[(s, c, h, cols.start)]
+            nc.vector.quantize_mx(out=cd[:, h, cols].bitcast(FP8X4), scales=sc[:, h, cols], in_=src[:].rearrange("p n t -> p (n t)"))
 
         def store(c, h, pair, share=False):
             for b in (2 * pair, 2 * pair + 1):
@@ -181,54 +177,54 @@ def tile_dense_heat_steps_t1_kernel(tc, q, w, heater, inv_cap, out):
                 copy(out=res[:].rearrange("p (m t) -> p m t", t=4), in_=bank[:].rearrange("p t m -> p m t"))
                 nc.sync.dma_start(out=hbm_rows(out, c)[:, b, 512 * h : 512 * (h + 1)], in_=res[:])
 
-        units = [(0, 0, 0), (0, 1, 0), (0, 0, 1), (0, 1, 1)]
-        for period in range(2, CHUNKS + 3):
-            for s, c in ((0, period), (1, period - 2), (2, period - 3)):
-                if 0 <= c < CHUNKS:
-                    units.extend([(s, c, 0), (s, c, 1)])
+        order = [(0, 0), (0, 1), (1, 0), (1, 1), (2, 0), (0, 2), (2, 1)]
+        units = [(s, c, h, WHOLE) for s, c in order for h in range(2)]
+        units += [(s, 2, h, cols) for s in (1, 2) for cols in PAIRS for h in range(2)]
 
-        turn_q(0, 0)
         group_w(0, 0, nc.vector.tensor_copy)
-        quantize_q(0)
+        turn_q(0, 0)
         quantize_w(0, 0)
-        group_w(0, 1, nc.scalar.copy, slice(2, 4))
-        group_w(0, 1, nc.vector.tensor_copy, slice(0, 2))
-        turn_q(1, 0)
+        group_w(0, 1, nc.vector.tensor_copy)
+        turn_q(0, 1)
+        for g in range(2):
+            quantize_q(0, g, PAIRS[0])
         quantize_w(0, 1)
         group_w(1, 0, nc.vector.tensor_copy)
-        quantize_q(1)
         group_w(1, 1, nc.scalar.copy)
-        nc.gpsimd.tensor_copy(out=inv[:], in_=inv16[:])
-        to_quantize = []
-        to_store = []
-        for i, (s, c, h) in enumerate(units):
-            for half in range(2):
-                multiply(s, c, h, (2 * half, 2 * half + 1))
-                quiet = s < 2 and (half == 1 or i == 0 or units[i - 1][0] < 2)
-                if to_quantize and to_quantize[0][0] <= i - 2 and (quiet or i >= len(units) - 4):
-                    unit = to_quantize.pop(0)[1:]
-                    quantize_state(*unit)
-                    if unit[:2] == (1, CHUNKS - 1):
-                        prescale(*unit[1:])
-            if i == 0:
-                quantize_w(1, 0)
+        for g in range(2):
+            quantize_q(0, g, PAIRS[1])
+        for t in range(4):
+            multiply(0, 0, 0, t, PAIRS[0])
+        quantize_w(1, 0)
+        for t in range(4):
+            multiply(0, 0, 0, t, PAIRS[1])
+            if t % 2:
+                turn_q(1, t // 2)
+            if t == 1:
                 quantize_w(1, 1)
-            if s == 0 and h == 1 and 1 <= c < CHUNKS - 2:
-                turn_q(c + 2, 0)
-            if i == 1:
-                turn_q(2, 0)
-            if i == 2:
-                quantize_q(2)
-            if s == 0 and h == 1 and 2 <= c < CHUNKS - 1:
-                quantize_q(c + 1)
-            if to_store and to_store[0][0] <= i - LAG:
-                store(*to_store.pop(0)[1:])
-            if i == len(units) - 2:
-                store(*to_store.pop(0)[1:])
+        group_state(*units[0])
+        nc.gpsimd.tensor_copy(out=inv[:], in_=inv16[:])
+        to_quantize = [0]
+        to_store = []
+        for i in range(1, len(units)):
+            s, c, h, cols = units[i]
+            for t in range(4):
+                multiply(s, c, h, t, cols)
+                if t in QSLOT.get(i, QDEF) and to_quantize and to_quantize[0] <= i - (2 if t < 3 else 1):
+                    unit = units[to_quantize.pop(0)]
+                    quantize_state(*unit)
+                if i == 1 and t < 2:
+                    quantize_q(1, t, WHOLE)
+                if (i, t) in QQC:
+                    quantize_q(2, QQC.index((i, t)), WHOLE)
+                if i in TQC and t == 3:
+                    turn_q(2, TQC.index(i))
+                for k in range(TSLOT.get(i, ()).count(t)):
+                    store(*to_store.pop(0))
             if s < 2:
-                group_state(s, c, h)
-                to_quantize.append((i, s, c, h))
+                group_state(s, c, h, cols)
+                to_quantize.append(i)
             else:
-                to_store.append((i, c, h, 0))
+                to_store.extend([(c, h, pair) for pair in range(2) if cols.start <= PAIRS[pair].start < cols.stop])
         for job in to_store:
-            store(*job[1:], True)
+            store(*job, True)

@@ -13,7 +13,6 @@ U8 = mybir.dt.uint8
 FP8X4 = mybir.dt.float8_e4m3fn_x4
 ADD = mybir.AluOpType.add
 MULT = mybir.AluOpType.mult
-COPY = mybir.ActivationFunctionType.Copy
 
 P = 128
 CHUNK = 512
@@ -21,11 +20,11 @@ CHUNKS = B // CHUNK
 WHOLE = slice(0, CHUNK)
 PAIRS = [slice(0, 256), slice(256, 512)]
 LAST = CHUNKS - 1
-TQC = (1, 3)
-QDEF = (0,)
-QQC = [(7, 3), (8, 0)]
-QSLOT = {8: (), 9: (), 10: (3,), 11: (1,), 12: (0,), 13: (0,)}
-TSLOT = {10: (3,), 11: (3,), 12: (1, 3), 14: (3,), 16: (3,), 17: (3,), 18: (3,), 19: (3,), 20: (3,), 21: (3,)}
+W_AT = [(0, 3), (1, 1)]
+TURN_Q_AT = [(1, 1), (1, 3), (2, 3), (4, 3)]
+QUANT_Q_AT = [(2, 0), (8, 3)]
+QUIET = (9, 11)
+FINISH_AT = {(11, 3): (0, 0, (0, 1, 2, 3)), (13, 3): (0, 1, (0, 1, 2, 3)), (15, 1): (1, 0, (0, 1)), (17, 3): (1, 0, (2, 3)), (18, 3): (1, 1, (0, 1)), (19, 3): (1, 1, (2, 3)), (20, 3): (2, 0, (0, 1)), (21, 3): (2, 1, (0, 1)), (22, 3): (2, 0, (2, 3))}
 
 
 def tile_dense_heat_steps_t1_kernel(tc, q, w, heater, inv_cap, out):
@@ -37,7 +36,6 @@ def tile_dense_heat_steps_t1_kernel(tc, q, w, heater, inv_cap, out):
         ctx.enter_context(tc.manual_schedule())
 
         ident = keep.tile([P, P], F32, name="ident")
-        warm = keep.tile([P, 1], F32, name="warm")
         heat = keep.tile([P, 2, 4], BF16, name="heat")
         inv16 = keep.tile([P, 2, 4], BF16, name="inv16")
         inv = keep.tile([P, 2, 4], F32, name="inv")
@@ -77,10 +75,10 @@ def tile_dense_heat_steps_t1_kernel(tc, q, w, heater, inv_cap, out):
         load_q(2, 0)
         load_q(2, 1)
         nc.sync.dma_start(out=inv16[:], in_=inv_cap.rearrange("(g p t) -> p g t", g=2, t=4))
-        nc.vector.memset(warm[:], 0.0)
-        nc.scalar.activation(warm[:], warm[:], COPY, scale=1.0)
 
         codes = {}
+        held = {}
+        turned = {}
         grouped = {}
         w_grouped = {}
 
@@ -103,15 +101,17 @@ def tile_dense_heat_steps_t1_kernel(tc, q, w, heater, inv_cap, out):
         def quantize_w(h, g):
             nc.vector.quantize_mx(out=w_codes[:, h, g, :].bitcast(FP8X4), scales=w_scales[:, h, g, :], in_=w_grouped[(h, g)][:])
 
-        def turn_q(c, pair):
-            for b in (2 * pair, 2 * pair + 1):
-                words = q_rows[(c, pair)][:, b % 2, :].bitcast(F32)
-                bank = psum.tile([P, 4, P], F32, name="bank")
-                for g in range(2):
-                    for u in range(2):
-                        nc.tensor.transpose(bank[:, 2 * g + u, :], words[:, 256 * g + u : 256 * (g + 1) : 2], ident[:])
-                dst = q_words[c][:, :, P * b : P * (b + 1), :].rearrange("p g n t -> p g (n t)").bitcast(F32)
-                nc.scalar.copy(out=dst.rearrange("p g (n u) -> p g n u", u=2), in_=bank[:].rearrange("p (g u) n -> p g n u", g=2))
+        def turn_q(c, b):
+            words = q_rows[(c, b // 2)][:, b % 2, :].bitcast(F32)
+            bank = psum.tile([P, 4, P], F32, name="bank")
+            for g in range(2):
+                for u in range(2):
+                    nc.tensor.transpose(bank[:, 2 * g + u, :], words[:, 256 * g + u : 256 * (g + 1) : 2], ident[:])
+            turned[(c, b)] = bank
+
+        def copy_q(c, b):
+            dst = q_words[c][:, :, P * b : P * (b + 1), :].rearrange("p g n t -> p g (n t)").bitcast(F32)
+            nc.scalar.copy(out=dst.rearrange("p g (n u) -> p g n u", u=2), in_=turned[(c, b)][:].rearrange("p (g u) n -> p g n u", g=2))
 
         def quantize_q(c, g, cols):
             cd, sc = codes_of(0, c)
@@ -130,11 +130,15 @@ def tile_dense_heat_steps_t1_kernel(tc, q, w, heater, inv_cap, out):
                 stop=(g == 1),
             )
 
-        def multiply(s, c, h, t, cols=WHOLE):
-            bank = psum.tile([P, CHUNK], F32, name="bank")
-            for g in range(2):
-                one_pass(bank, s, c, h, t, g, cols)
-            advance(bank, s, c, h, t, cols)
+        def multiply(s, c, h, k, cols, n):
+            if k % n == 0:
+                for t in range(k, k + n):
+                    bank = psum.tile([P, CHUNK], F32, name="bank")
+                    for g in range(2):
+                        one_pass(bank, s, c, h, t, g, cols)
+                    held[t] = bank
+            t = k - k % n + n - 1 - k % n
+            advance(held[t], s, c, h, t, cols)
 
         def advance(bank, s, c, h, t, cols):
             now = state[c][h][:, t, cols]
@@ -167,25 +171,42 @@ def tile_dense_heat_steps_t1_kernel(tc, q, w, heater, inv_cap, out):
             src = grouped[(s, c, h, cols.start)]
             nc.vector.quantize_mx(out=cd[:, h, cols].bitcast(FP8X4), scales=sc[:, h, cols], in_=src[:].rearrange("p n t -> p (n t)"))
 
-        def store(c, h, pair, share=False):
-            for b in (2 * pair, 2 * pair + 1):
-                bank = psum.tile([P, 4, P], F32, name="bank")
-                for t in range(4):
-                    nc.tensor.transpose(bank[:, t, :], state[c][h][:, t, P * b : P * (b + 1)], ident[:])
-                res = stage.tile([P, 512], F32, name="res", bufs=8)
-                copy = nc.vector.tensor_copy if share and b % 2 else nc.scalar.copy
-                copy(out=res[:].rearrange("p (m t) -> p m t", t=4), in_=bank[:].rearrange("p t m -> p m t"))
-                nc.sync.dma_start(out=hbm_rows(out, c)[:, b, 512 * h : 512 * (h + 1)], in_=res[:])
+        def turn_out(c, h, b):
+            bank = psum.tile([P, 4, P], F32, name="bank")
+            for t in range(4):
+                nc.tensor.transpose(bank[:, t, :], state[c][h][:, t, P * b : P * (b + 1)], ident[:])
+            turned[(c, h, b)] = bank
+
+        def store(c, h, b, copy):
+            res = stage.tile([P, 512], F32, name="res", bufs=8)
+            copy(out=res[:].rearrange("p (m t) -> p m t", t=4), in_=turned[(c, h, b)][:].rearrange("p t m -> p m t"))
+            nc.sync.dma_start(out=hbm_rows(out, c)[:, b, 512 * h : 512 * (h + 1)], in_=res[:])
 
         order = [(0, 0), (0, 1), (1, 0), (1, 1), (2, 0), (0, 2), (2, 1)]
-        units = [(s, c, h, WHOLE) for s, c in order for h in range(2)]
-        units += [(s, 2, h, cols) for s in (1, 2) for cols in PAIRS for h in range(2)]
+        units = [(0, 0, 0, cols) for cols in PAIRS] + [(s, c, h, WHOLE) for s, c in order for h in range(2)][1:]
+        units += [(s, LAST, h, cols) for s in (1, 2) for cols in PAIRS for h in range(2)]
+
+        def turn_q_pair(c, pair):
+            for b in (2 * pair, 2 * pair + 1):
+                turn_q(c, b)
+            for b in (2 * pair + 1, 2 * pair):
+                copy_q(c, b)
+
+        def finish(c, h, blocks, share=False):
+            for b in blocks:
+                turn_out(c, h, b)
+            for b in blocks:
+                store(c, h, b, nc.vector.tensor_copy if share and b % 2 else nc.scalar.copy)
 
         group_w(0, 0, nc.vector.tensor_copy)
-        turn_q(0, 0)
+        for b in range(2):
+            turn_q(0, b)
+            copy_q(0, b)
         quantize_w(0, 0)
         group_w(0, 1, nc.vector.tensor_copy)
-        turn_q(0, 1)
+        for b in range(2, 4):
+            turn_q(0, b)
+            copy_q(0, b)
         for g in range(2):
             quantize_q(0, g, PAIRS[0])
         quantize_w(0, 1)
@@ -193,38 +214,26 @@ def tile_dense_heat_steps_t1_kernel(tc, q, w, heater, inv_cap, out):
         group_w(1, 1, nc.scalar.copy)
         for g in range(2):
             quantize_q(0, g, PAIRS[1])
-        for t in range(4):
-            multiply(0, 0, 0, t, PAIRS[0])
-        quantize_w(1, 0)
-        for t in range(4):
-            multiply(0, 0, 0, t, PAIRS[1])
-            if t % 2:
-                turn_q(1, t // 2)
-            if t == 1:
-                quantize_w(1, 1)
-        group_state(*units[0])
         nc.gpsimd.tensor_copy(out=inv[:], in_=inv16[:])
-        to_quantize = [0]
-        to_store = []
-        for i in range(1, len(units)):
-            s, c, h, cols = units[i]
-            for t in range(4):
-                multiply(s, c, h, t, cols)
-                if t in QSLOT.get(i, QDEF) and to_quantize and to_quantize[0] <= i - (2 if t < 3 else 1):
-                    unit = units[to_quantize.pop(0)]
-                    quantize_state(*unit)
-                if i == 1 and t < 2:
-                    quantize_q(1, t, WHOLE)
-                if (i, t) in QQC:
-                    quantize_q(2, QQC.index((i, t)), WHOLE)
-                if i in TQC and t == 3:
-                    turn_q(2, TQC.index(i))
-                for k in range(TSLOT.get(i, ()).count(t)):
-                    store(*to_store.pop(0))
-            if s < 2:
-                group_state(s, c, h, cols)
-                to_quantize.append(i)
-            else:
-                to_store.extend([(c, h, pair) for pair in range(2) if cols.start <= PAIRS[pair].start < cols.stop])
-        for job in to_store:
-            store(*job, True)
+        waiting = []
+        for i, (s, c, h, cols) in enumerate(units):
+            for k in range(4):
+                multiply(s, c, h, k, cols, 1 if i < 3 else 2)
+                if (i, k) in W_AT:
+                    quantize_w(1, W_AT.index((i, k)))
+                if (i, k) in TURN_Q_AT:
+                    n = TURN_Q_AT.index((i, k))
+                    turn_q_pair(1 + n // 2, n % 2)
+                if (i, k) in QUANT_Q_AT:
+                    for g in range(2):
+                        quantize_q(1 + QUANT_Q_AT.index((i, k)), g, WHOLE)
+                if (i, k) in FINISH_AT:
+                    finish(*FINISH_AT[(i, k)])
+                if k == 0 and not QUIET[0] <= i <= QUIET[1] or (i, k) == (QUIET[1], 3):
+                    for j in [j for j in waiting if j <= i - 2]:
+                        waiting.remove(j)
+                        quantize_state(*units[j][:3], WHOLE if j == 1 else units[j][3])
+            if s < 2 and i > 0:
+                group_state(s, c, h, WHOLE if i == 1 else cols)
+                waiting.append(i)
+        finish(LAST, 1, (2, 3), True)

@@ -89,13 +89,12 @@ def tile_dense_heat_steps_t1_kernel(tc, q, w, heater, inv_cap, out):
                 codes[(s, c)] = (cd, sc)
             return codes[(s, c)]
 
-        def group_w(h, g, copy, ts=slice(0, 4)):
-            if (h, g) not in w_grouped:
-                dst = stage.tile([P, 2048], BF16, name="half", align_bytes=256, bufs=8)
-                w_grouped[(h, g)] = dst
+        def group_w(h, g, copy):
+            dst = stage.tile([P, 2048], BF16, name="half", align_bytes=256, bufs=8)
+            w_grouped[(h, g)] = dst
             copy(
-                out=w_grouped[(h, g)][:].rearrange("p (t m j) -> p t m j", t=4, j=4)[:, ts],
-                in_=w_rows[(h, g)][:].rearrange("p j (m t) -> p t m j", t=4)[:, ts],
+                out=dst[:].rearrange("p (t m i j) -> p m t i j", t=4, i=2, j=4),
+                in_=w_rows[(h, g)][:].rearrange("p j (m i t) -> p m t i j", t=4, i=2),
             )
 
         def quantize_w(h, g):
@@ -116,6 +115,14 @@ def tile_dense_heat_steps_t1_kernel(tc, q, w, heater, inv_cap, out):
         def quantize_q(c, g, cols):
             cd, sc = codes_of(0, c)
             nc.vector.quantize_mx(out=cd[:, g, cols].bitcast(FP8X4), scales=sc[:, g, cols], in_=q_words[c][:, g, cols, :].rearrange("p n t -> p (n t)"))
+
+        def quantize_q_whole(c):
+            cd, sc = codes_of(0, c)
+            nc.vector.quantize_mx(
+                out=cd[:].rearrange("p g n -> p (g n)").bitcast(FP8X4),
+                scales=sc[:].rearrange("p g n -> p (g n)"),
+                in_=q_words[c][:].rearrange("p g n t -> p (g n t)"),
+            )
 
         def one_pass(bank, s, c, h, t, g, cols):
             cd, sc = codes_of(s, c)
@@ -171,11 +178,13 @@ def tile_dense_heat_steps_t1_kernel(tc, q, w, heater, inv_cap, out):
             src = grouped[(s, c, h, cols.start)]
             nc.vector.quantize_mx(out=cd[:, h, cols].bitcast(FP8X4), scales=sc[:, h, cols], in_=src[:].rearrange("p n t -> p (n t)"))
 
-        def turn_out(c, h, b):
-            bank = psum.tile([P, 4, P], F32, name="bank")
-            for t in range(4):
-                nc.tensor.transpose(bank[:, t, :], state[c][h][:, t, P * b : P * (b + 1)], ident[:])
-            turned[(c, h, b)] = bank
+        def turn_out(c, h, blocks, by_tile):
+            for b in blocks:
+                bank = psum.tile([P, 4, P], F32, name="bank")
+                turned[(c, h, b)] = bank
+            steps = [(b, t) for t in (1, 0, 3, 2) for b in blocks] if by_tile else [(b, t) for b in blocks for t in range(4)]
+            for b, t in steps:
+                nc.tensor.transpose(turned[(c, h, b)][:, t, :], state[c][h][:, t, P * b : P * (b + 1)], ident[:])
 
         def store(c, h, b, copy):
             res = stage.tile([P, 512], F32, name="res", bufs=8)
@@ -193,8 +202,7 @@ def tile_dense_heat_steps_t1_kernel(tc, q, w, heater, inv_cap, out):
                 copy_q(c, b)
 
         def finish(c, h, blocks, share=False):
-            for b in blocks:
-                turn_out(c, h, b)
+            turn_out(c, h, blocks, share)
             for b in blocks:
                 store(c, h, b, nc.vector.tensor_copy if share and b % 2 else nc.scalar.copy)
 
@@ -225,8 +233,7 @@ def tile_dense_heat_steps_t1_kernel(tc, q, w, heater, inv_cap, out):
                     n = TURN_Q_AT.index((i, k))
                     turn_q_pair(1 + n // 2, n % 2)
                 if (i, k) in QUANT_Q_AT:
-                    for g in range(2):
-                        quantize_q(1 + QUANT_Q_AT.index((i, k)), g, WHOLE)
+                    quantize_q_whole(1 + QUANT_Q_AT.index((i, k)))
                 if (i, k) in FINISH_AT:
                     finish(*FINISH_AT[(i, k)])
                 if k == 0 and not QUIET[0] <= i <= QUIET[1] or (i, k) == (QUIET[1], 3):

@@ -186,10 +186,10 @@ def tile_dense_heat_steps_t1_kernel(tc, q, w, heater, inv_cap, out):
             for b, t in steps:
                 nc.tensor.transpose(turned[(c, h, b)][:, t, :], state[c][h][:, t, P * b : P * (b + 1)], ident[:])
 
-        def store(c, h, b, copy):
+        def store(c, h, b, copy, queue):
             res = stage.tile([P, 512], F32, name="res", bufs=8)
             copy(out=res[:].rearrange("p (m t) -> p m t", t=4), in_=turned[(c, h, b)][:].rearrange("p t m -> p m t"))
-            nc.sync.dma_start(out=hbm_rows(out, c)[:, b, 512 * h : 512 * (h + 1)], in_=res[:])
+            queue.dma_start(out=hbm_rows(out, c)[:, b, 512 * h : 512 * (h + 1)], in_=res[:])
 
         order = [(0, 0), (0, 1), (1, 0), (1, 1), (2, 0), (0, 2), (2, 1)]
         units = [(0, 0, 0, cols) for cols in PAIRS] + [(s, c, h, WHOLE) for s, c in order for h in range(2)][1:]
@@ -204,7 +204,10 @@ def tile_dense_heat_steps_t1_kernel(tc, q, w, heater, inv_cap, out):
         def finish(c, h, blocks, share=False):
             turn_out(c, h, blocks, share)
             for b in blocks:
-                store(c, h, b, nc.vector.tensor_copy if share and b % 2 else nc.scalar.copy)
+                if share and b % 2:
+                    store(c, h, b, nc.vector.tensor_copy, nc.sync)
+                else:
+                    store(c, h, b, nc.scalar.copy, nc.scalar if share else nc.sync)
 
         group_w(0, 0, nc.vector.tensor_copy)
         for b in range(2):

@@ -24,7 +24,7 @@ W_AT = [(0, 3), (1, 1)]
 TURN_Q_AT = [(1, 1), (1, 3), (2, 3), (4, 3)]
 QUANT_Q_AT = [(2, 0), (8, 3)]
 QUIET = (9, 11)
-FINISH_AT = {(11, 3): (0, 0, (0, 1, 2, 3)), (13, 3): (0, 1, (0, 1, 2, 3)), (15, 1): (1, 0, (0, 1)), (17, 3): (1, 0, (2, 3)), (18, 3): (1, 1, (0, 1)), (19, 3): (1, 1, (2, 3)), (20, 3): (2, 0, (0, 1)), (21, 3): (2, 1, (0, 1)), (22, 3): (2, 0, (2, 3))}
+FINISH_AT = {(11, 3): (0, 0, (0, 1, 2, 3)), (13, 3): (0, 1, (0, 1, 2, 3)), (15, 3): (1, 0, (0, 1)), (17, 3): (1, 0, (2, 3)), (18, 3): (1, 1, (0, 1)), (19, 3): (1, 1, (2, 3)), (20, 3): (2, 0, (0, 1)), (21, 3): (2, 1, (0, 1)), (22, 3): (2, 0, (2, 3))}
 
 
 def tile_dense_heat_steps_t1_kernel(tc, q, w, heater, inv_cap, out):

@@ -32,7 +32,7 @@ def tile_dense_heat_steps_t1_kernel(tc, q, w, heater, inv_cap, out):
     with ExitStack() as ctx:
         keep = ctx.enter_context(tc.tile_pool(name="keep", bufs=1))
         stage = ctx.enter_context(tc.tile_pool(name="stage", bufs=4))
-        psum = ctx.enter_context(tc.psum_pool(name="psum", bufs=8))
+        psum = ctx.enter_context(tc.psum_pool(name="psum", bufs=1))
         ctx.enter_context(tc.manual_schedule())
 
         ident = keep.tile([P, P], F32, name="ident")
@@ -78,6 +78,18 @@ def tile_dense_heat_steps_t1_kernel(tc, q, w, heater, inv_cap, out):
 
         codes = {}
         held = {}
+        free = list(range(8))
+        number = {}
+
+        def take(key, shape):
+            n = free.pop(0)
+            number[key] = n
+            bank = psum.tile(shape, F32, name="bank%d" % n)
+            return bank
+
+        def give(key):
+            free.append(number.pop(key))
+
         turned = {}
         grouped = {}
         w_grouped = {}
@@ -102,7 +114,7 @@ def tile_dense_heat_steps_t1_kernel(tc, q, w, heater, inv_cap, out):
 
         def turn_q(c, b):
             words = q_rows[(c, b // 2)][:, b % 2, :].bitcast(F32)
-            bank = psum.tile([P, 4, P], F32, name="bank")
+            bank = take((c, b), [P, 4, P])
             for g in range(2):
                 for u in range(2):
                     nc.tensor.transpose(bank[:, 2 * g + u, :], words[:, 256 * g + u : 256 * (g + 1) : 2], ident[:])
@@ -111,6 +123,7 @@ def tile_dense_heat_steps_t1_kernel(tc, q, w, heater, inv_cap, out):
         def copy_q(c, b):
             dst = q_words[c][:, :, P * b : P * (b + 1), :].rearrange("p g n t -> p g (n t)").bitcast(F32)
             nc.scalar.copy(out=dst.rearrange("p g (n u) -> p g n u", u=2), in_=turned[(c, b)][:].rearrange("p (g u) n -> p g n u", g=2))
+            give((c, b))
 
         def quantize_q(c, g, cols):
             cd, sc = codes_of(0, c)
@@ -140,12 +153,13 @@ def tile_dense_heat_steps_t1_kernel(tc, q, w, heater, inv_cap, out):
         def multiply(s, c, h, k, cols, n):
             if k % n == 0:
                 for t in range(k, k + n):
-                    bank = psum.tile([P, CHUNK], F32, name="bank")
+                    bank = take(t, [P, CHUNK])
                     for g in range(2):
                         one_pass(bank, s, c, h, t, g, cols)
                     held[t] = bank
             t = k - k % n + n - 1 - k % n
             advance(held[t], s, c, h, t, cols)
+            give(t)
 
         def advance(bank, s, c, h, t, cols):
             now = state[c][h][:, t, cols]
@@ -180,8 +194,7 @@ def tile_dense_heat_steps_t1_kernel(tc, q, w, heater, inv_cap, out):
 
         def turn_out(c, h, blocks, by_tile):
             for b in blocks:
-                bank = psum.tile([P, 4, P], F32, name="bank")
-                turned[(c, h, b)] = bank
+                turned[(c, h, b)] = take((c, h, b), [P, 4, P])
             steps = [(b, t) for t in (1, 0, 3, 2) for b in blocks] if by_tile else [(b, t) for b in blocks for t in range(4)]
             for b, t in steps:
                 nc.tensor.transpose(turned[(c, h, b)][:, t, :], state[c][h][:, t, P * b : P * (b + 1)], ident[:])
@@ -189,6 +202,7 @@ def tile_dense_heat_steps_t1_kernel(tc, q, w, heater, inv_cap, out):
         def store(c, h, b, copy, queue):
             res = stage.tile([P, 512], F32, name="res", bufs=8)
             copy(out=res[:].rearrange("p (m t) -> p m t", t=4), in_=turned[(c, h, b)][:].rearrange("p t m -> p m t"))
+            give((c, h, b))
             queue.dma_start(out=hbm_rows(out, c)[:, b, 512 * h : 512 * (h + 1)], in_=res[:])
 
         order = [(0, 0), (0, 1), (1, 0), (1, 1), (2, 0), (0, 2), (2, 1)]

@@ -15,16 +15,30 @@ ADD = mybir.AluOpType.add
 MULT = mybir.AluOpType.mult
 
 P = 128
-CHUNK = 512
-CHUNKS = B // CHUNK
-WHOLE = slice(0, CHUNK)
-PAIRS = [slice(0, 256), slice(256, 512)]
+PAIR = 256
+WIDTH = [256, 512, 512, 256]
+CHUNKS = len(WIDTH)
+FIRST = [sum(WIDTH[:c]) // PAIR for c in range(CHUNKS)]
 LAST = CHUNKS - 1
-W_AT = [(0, 3), (1, 1)]
-TURN_Q_AT = [(1, 1), (1, 3), (2, 3), (4, 3)]
-QUANT_Q_AT = [(2, 0), (8, 3)]
-QUIET = (9, 11)
-FINISH_AT = {(11, 3): (0, 0, (0, 1, 2, 3)), (13, 3): (0, 1, (0, 1, 2, 3)), (15, 3): (1, 0, (0, 1)), (17, 3): (1, 0, (2, 3)), (18, 3): (1, 1, (0, 1)), (19, 3): (1, 1, (2, 3)), (20, 3): (2, 0, (0, 1)), (21, 3): (2, 1, (0, 1)), (22, 3): (2, 0, (2, 3))}
+ORDER = [(0, 0), (0, 1), (1, 0), (1, 1), (2, 0), (0, 2), (2, 1), (1, 2), (0, 3), (2, 2), (1, 3), (2, 3)]
+AFTER_M = {(0,3):[("tp",1,1)],(1,3):[("tp",2,0)],(4,3):[("tp",2,1)],(7,1):[("tp",3,0)],(11,1):[("fin",0,0,(0,1))],(12,3):[("fin",0,1,(0,1))],(14,1):[("fin",1,0,(0,1))],(14,3):[("fin",1,0,(2,3))],(16,1):[("fin",1,1,(0,1))],(18,3):[("fin",1,1,(2,3))],(20,3):[("fin",2,0,(0,1))],(21,1):[("fin",2,0,(2,3))],(21,3):[("F",2,1,(0,1)),("F",2,1,(2,3))],(23,3):[("fin",3,0,(0,1),"SS"),("fin",3,1,(0,1),"SV",True)]}
+AFTER_A = {(0,1):[("qw",1,0,2,4)],(0,3):[("qw",1,1,2,4),("gs",0,0,0,"S")],(1,1):[("qq",1)],(1,3):[("qs",0,0,0),("gs",0,0,1,"S")],
+(2,3):[("qs",0,0,1),("gs",0,1,0,"S",0,256),("gs",0,1,0,"G",256,512)],(3,3):[("qs",0,1,0),("gs",0,1,1,"S",0,256),("gs",0,1,1,"G",256,512)],
+(4,3):[("gs",1,0,0,"S")],(5,3):[("qs",0,1,1),("gs",1,0,1,"S"),("qq",2),("qs",1,0,0)],
+(6,3):[("qs",1,0,1),("gs",1,1,0,"S",0,256),("gs",1,1,0,"G",256,512)],(7,3):[("qs",1,1,0),("gs",1,1,1,"S",0,256),("gs",1,1,1,"G",256,512)],
+(9,3):[("qq",3),("qs",1,1,1)],(10,3):[("gs",0,2,0,"S",0,256),("gs",0,2,0,"G",256,512)],(11,3):[("qs",0,2,0),("gs",0,2,1,"S",0,256),("gs",0,2,1,"G",256,512)],
+(12,3):[("qs",0,2,1)],(14,3):[("gs",1,2,0,"S",0,256),("gs",1,2,0,"G",256,512)],(15,3):[("qs",1,2,0),("gs",1,2,1,"S",0,256),("gs",1,2,1,"G",256,512)],
+(16,3):[("gs",0,3,0,"S")],(17,3):[("qs",1,2,1),("gs",0,3,1,"S"),("qs",0,3,0)],(18,3):[("qs",0,3,1)],
+(20,3):[("gs",1,3,0,"S"),("sc",3,0,"G",0,2),("sc",3,0,"S",2,4)],(21,3):[("qs",1,3,0),("gs",1,3,1,"V"),("sc",3,1,"V",0,2),("qs",1,3,1),("sc",3,1,"V",2,4),("O",2,1,(0,1),"SS"),("O",2,1,(2,3),"SS")]}
+SPLIT = (0, 6, 18, 22)
+DELAY = 3
+LEAD = 3
+ON_G = (0, 1)
+VIA_S = ()
+LOADS = [(0, 0), (0,), (0, 1), (1, 0), (1,), (1, 1), (2,), (3,), (4,), (5,)]
+HEAD = [("gw",0,0,"V",0,2),("gw",0,0,"S",2,4),("tq",0,0),("cq",0,0),("tq",0,1),("cq",0,1),("qw",0,0),("gw",0,1,"V"),("gw",1,0,"V",0,2),("qq",0),("qw",0,1),("gw",1,0,"S",2,4),("gw",1,1,"S",2,4),("T",1,0),("C",1,0),("gw",1,1,"V",0,2),("qw",1,0,0,2),("qw",1,1,0,2),("wid",)]
+TAIL = []
+EARLY_SCALE = [3]
 
 
 def tile_dense_heat_steps_t1_kernel(tc, q, w, heater, inv_cap, out):
@@ -41,20 +55,20 @@ def tile_dense_heat_steps_t1_kernel(tc, q, w, heater, inv_cap, out):
         inv = keep.tile([P, 2, 4], F32, name="inv")
         w_codes = keep.tile([P, 2, 2, 512], U32, name="w_codes", align_bytes=256)
         w_scales = keep.tile([P, 2, 2, 512], U8, name="w_scales", align_bytes=256)
-        q_words = [keep.tile([P, 2, CHUNK, 4], BF16, name="q_words%d" % c, align_bytes=256) for c in range(CHUNKS)]
-        state = [[keep.tile([P, 4, CHUNK], F32, name="state%d%d" % (c, h)) for h in range(2)] for c in range(CHUNKS)]
-        scaled = [keep.tile([P, 4, CHUNK], F32, name="scaled%d" % h) for h in range(2)]
+        q_words = [keep.tile([P, 2, WIDTH[c], 4], BF16, name="q_words%d" % c, align_bytes=256) for c in range(CHUNKS)]
+        state = [[keep.tile([P, 4, WIDTH[c]], F32, name="state%d%d" % (c, h)) for h in range(2)] for c in range(CHUNKS)]
+        scaled = {(c, h): keep.tile([P, 4, WIDTH[c]], F32, name="scaled%d%d" % (c, h)) for h in range(2) for c in EARLY_SCALE}
 
-        def hbm_rows(x, c):
-            return x[CHUNK * c : CHUNK * (c + 1), :].rearrange("(p b) k -> p b k", b=4)
+        def hbm_rows(x, j):
+            return x[PAIR * j : PAIR * (j + 1), :].rearrange("(p b) k -> p b k", b=2)
 
         q_rows = {}
         w_rows = {}
 
-        def load_q(c, pair):
-            rows = keep.tile([P, 2, N], BF16, name="q_rows%d%d" % (c, pair), align_bytes=256)
-            nc.sync.dma_start(out=rows[:], in_=hbm_rows(q, c)[:, 2 * pair : 2 * pair + 2, :])
-            q_rows[(c, pair)] = rows
+        def load_q(j):
+            rows = keep.tile([P, 2, N], BF16, name="q_rows%d" % j, align_bytes=256)
+            nc.sync.dma_start(out=rows[:], in_=hbm_rows(q, j))
+            q_rows[j] = rows
 
         def load_w(h, g):
             rows = stage.tile([P, 4, 512], BF16, name="half", align_bytes=256, bufs=8)
@@ -64,16 +78,11 @@ def tile_dense_heat_steps_t1_kernel(tc, q, w, heater, inv_cap, out):
 
         make_identity(nc, ident[:])
         nc.scalar.dma_start(out=heat[:], in_=heater.rearrange("(g p t) -> p g t", g=2, t=4))
-        load_w(0, 0)
-        load_q(0, 0)
-        load_w(0, 1)
-        load_q(0, 1)
-        load_w(1, 0)
-        load_w(1, 1)
-        load_q(1, 0)
-        load_q(1, 1)
-        load_q(2, 0)
-        load_q(2, 1)
+        for x in LOADS:
+            if len(x) == 1:
+                load_q(*x)
+            else:
+                load_w(*x)
         nc.sync.dma_start(out=inv16[:], in_=inv_cap.rearrange("(g p t) -> p g t", g=2, t=4))
 
         codes = {}
@@ -94,42 +103,60 @@ def tile_dense_heat_steps_t1_kernel(tc, q, w, heater, inv_cap, out):
         grouped = {}
         w_grouped = {}
 
+        def on_gpsimd(out, in_):
+            nc.gpsimd.tensor_scalar(out, in_, 1.0, 0.0, MULT, ADD)
+
+        copier = {"V": nc.vector.tensor_copy, "S": nc.scalar.copy, "G": on_gpsimd}
+
         def codes_of(s, c):
             if (s, c) not in codes:
-                cd = keep.tile([P, 2, CHUNK], U32, name="codes%d%d" % (s % 2, c), align_bytes=256)
-                sc = keep.tile([P, 2, CHUNK], U8, name="scales%d%d" % (s % 2, c), align_bytes=256)
+                cd = keep.tile([P, 2, WIDTH[c]], U32, name="codes%d%d" % (s % 2, c), align_bytes=256)
+                sc = keep.tile([P, 2, WIDTH[c]], U8, name="scales%d%d" % (s % 2, c), align_bytes=256)
                 codes[(s, c)] = (cd, sc)
             return codes[(s, c)]
 
-        def group_w(h, g, copy):
-            dst = stage.tile([P, 2048], BF16, name="half", align_bytes=256, bufs=8)
-            w_grouped[(h, g)] = dst
-            copy(
-                out=dst[:].rearrange("p (t m i j) -> p m t i j", t=4, i=2, j=4),
-                in_=w_rows[(h, g)][:].rearrange("p j (m i t) -> p m t i j", t=4, i=2),
+        def group_w(h, g, e, t0=0, t1=4):
+            if (h, g) not in w_grouped:
+                w_grouped[(h, g)] = stage.tile([P, 2048], BF16, name="half", align_bytes=256, bufs=8)
+            dst = w_grouped[(h, g)]
+            if e == "G":
+                copier[e](
+                    out=dst[:].rearrange("p (t m j) -> p t m j", t=4, j=4)[:, t0:t1],
+                    in_=w_rows[(h, g)][:].rearrange("p j (m t) -> p t m j", t=4)[:, t0:t1],
+                )
+            else:
+                copier[e](
+                    out=dst[:].rearrange("p (t m i j) -> p m t i j", t=4, i=2, j=4)[:, :, t0:t1],
+                    in_=w_rows[(h, g)][:].rearrange("p j (m i t) -> p m t i j", t=4, i=2)[:, :, t0:t1],
+                )
+
+        def quantize_w(h, g, t0=0, t1=4):
+            nc.vector.quantize_mx(
+                out=w_codes[:, h, g, P * t0 : P * t1].bitcast(FP8X4),
+                scales=w_scales[:, h, g, P * t0 : P * t1],
+                in_=w_grouped[(h, g)][:, 512 * t0 : 512 * t1],
             )
 
-        def quantize_w(h, g):
-            nc.vector.quantize_mx(out=w_codes[:, h, g, :].bitcast(FP8X4), scales=w_scales[:, h, g, :], in_=w_grouped[(h, g)][:])
-
         def turn_q(c, b):
-            words = q_rows[(c, b // 2)][:, b % 2, :].bitcast(F32)
+            words = q_rows[FIRST[c] + b // 2][:, b % 2, :].bitcast(F32)
             bank = take((c, b), [P, 4, P])
             for g in range(2):
                 for u in range(2):
                     nc.tensor.transpose(bank[:, 2 * g + u, :], words[:, 256 * g + u : 256 * (g + 1) : 2], ident[:])
             turned[(c, b)] = bank
 
-        def copy_q(c, b):
+        def copy_q(c, b, e="S"):
             dst = q_words[c][:, :, P * b : P * (b + 1), :].rearrange("p g n t -> p g (n t)").bitcast(F32)
-            nc.scalar.copy(out=dst.rearrange("p g (n u) -> p g n u", u=2), in_=turned[(c, b)][:].rearrange("p (g u) n -> p g n u", g=2))
+            copier[e](out=dst.rearrange("p g (n u) -> p g n u", u=2), in_=turned[(c, b)][:].rearrange("p (g u) n -> p g n u", g=2))
             give((c, b))
 
-        def quantize_q(c, g, cols):
-            cd, sc = codes_of(0, c)
-            nc.vector.quantize_mx(out=cd[:, g, cols].bitcast(FP8X4), scales=sc[:, g, cols], in_=q_words[c][:, g, cols, :].rearrange("p n t -> p (n t)"))
+        def turn_q_pair(c, pair):
+            for b in (2 * pair, 2 * pair + 1):
+                turn_q(c, b)
+            for b in (2 * pair, 2 * pair + 1):
+                copy_q(c, b)
 
-        def quantize_q_whole(c):
+        def quantize_q(c):
             cd, sc = codes_of(0, c)
             nc.vector.quantize_mx(
                 out=cd[:].rearrange("p g n -> p (g n)").bitcast(FP8X4),
@@ -137,127 +164,192 @@ def tile_dense_heat_steps_t1_kernel(tc, q, w, heater, inv_cap, out):
                 in_=q_words[c][:].rearrange("p g n t -> p (g n t)"),
             )
 
-        def one_pass(bank, s, c, h, t, g, cols):
+        def one_pass(bank, s, c, h, t, g):
             cd, sc = codes_of(s, c)
             cells = slice(P * t, P * (t + 1))
             nc.tensor.matmul_mx(
-                out=bank[:, cols],
+                out=bank[:],
                 lhsT=w_codes[:, h, g, cells].bitcast(FP8X4),
                 lhsT_scale=w_scales[:, h, g, cells],
-                rhs=cd[:, g, cols].bitcast(FP8X4),
-                rhs_scale=sc[:, g, cols],
+                rhs=cd[:, g, :].bitcast(FP8X4),
+                rhs_scale=sc[:, g, :],
                 start=(g == 0),
                 stop=(g == 1),
             )
 
-        def multiply(s, c, h, k, cols, n):
-            if k % n == 0:
-                for t in range(k, k + n):
-                    bank = take(t, [P, CHUNK])
-                    for g in range(2):
-                        one_pass(bank, s, c, h, t, g, cols)
-                    held[t] = bank
-            t = k - k % n + n - 1 - k % n
-            advance(held[t], s, c, h, t, cols)
+        def multiply(s, c, h, t, split):
+            if split and t == 0:
+                for u in range(4):
+                    held[u] = take(u, [P, WIDTH[c]])
+                    one_pass(held[u], s, c, h, u, 0)
+            if not split:
+                held[t] = take(t, [P, WIDTH[c]])
+                one_pass(held[t], s, c, h, t, 0)
+            one_pass(held[t], s, c, h, t, 1)
+            advance(held[t], s, c, h, t)
             give(t)
 
-        def advance(bank, s, c, h, t, cols):
-            now = state[c][h][:, t, cols]
-            if s == 0:
-                nc.vector.scalar_tensor_tensor(now, bank[:, cols], heat[:, h, t : t + 1], q_words[c][:, h, cols, t], ADD, ADD)
+        def advance(bank, s, c, h, t):
+            now = state[c][h][:, t, :]
+            if (s, c, h, t) in VIA_S:
+                part = stage.tile([P, WIDTH[c]], F32, name="part", bufs=2)
+                if s < 2:
+                    nc.scalar.activation(part[:], bank[:], mybir.ActivationFunctionType.Identity, bias=heat[:, h, t : t + 1])
+                else:
+                    nc.scalar.copy(part[:], bank[:])
+                nc.gpsimd.tensor_tensor(now, part[:], q_words[c][:, h, :, t] if s == 0 else now, ADD)
+                if s == 2:
+                    nc.gpsimd.tensor_scalar(now, now, inv[:, h, t : t + 1], 0.0, MULT, ADD)
+            elif s == 0:
+                nc.vector.scalar_tensor_tensor(now, bank[:], heat[:, h, t : t + 1], q_words[c][:, h, :, t], ADD, ADD)
             elif s == 1:
-                nc.vector.scalar_tensor_tensor(now, bank[:, cols], heat[:, h, t : t + 1], now, ADD, ADD)
-                if c == LAST:
-                    nc.gpsimd.tensor_scalar(scaled[h][:, t, cols], now, inv[:, h, t : t + 1], 0.0, MULT, ADD)
-            elif c == LAST:
-                nc.vector.scalar_tensor_tensor(now, bank[:, cols], inv[:, h, t : t + 1], scaled[h][:, t, cols], MULT, ADD)
+                nc.vector.scalar_tensor_tensor(now, bank[:], heat[:, h, t : t + 1], now, ADD, ADD)
+            elif c in EARLY_SCALE:
+                nc.vector.scalar_tensor_tensor(now, bank[:], inv[:, h, t : t + 1], scaled[(c, h)][:, t, :], MULT, ADD)
             else:
-                nc.vector.tensor_tensor(now, bank[:, cols], now, ADD)
-                scale(c, h, t, cols)
+                nc.vector.tensor_tensor(now, bank[:], now, ADD)
+                if t in ON_G:
+                    nc.gpsimd.tensor_scalar(now, now, inv[:, h, t : t + 1], 0.0, MULT, ADD)
+                else:
+                    nc.scalar.mul(now, now, inv[:, h, t : t + 1])
 
-        def scale(c, h, t, cols):
-            now = state[c][h][:, t, cols]
-            nc.gpsimd.tensor_scalar(now, now, inv[:, h, t : t + 1], 0.0, MULT, ADD)
+        def scale(c, h, e, t0=0, t1=4):
+            for t in range(t0, t1):
+                if e == "S":
+                    nc.scalar.mul(scaled[(c, h)][:, t, :], state[c][h][:, t, :], inv[:, h, t : t + 1])
+                elif e == "V":
+                    nc.vector.tensor_scalar(scaled[(c, h)][:, t, :], state[c][h][:, t, :], inv[:, h, t : t + 1], 0.0, MULT, ADD)
+                else:
+                    nc.gpsimd.tensor_scalar(scaled[(c, h)][:, t, :], state[c][h][:, t, :], inv[:, h, t : t + 1], 0.0, MULT, ADD)
 
-        def group_state(s, c, h, cols):
-            dst = stage.tile([P, cols.stop - cols.start, 4], BF16, name="half", align_bytes=256, bufs=8)
-            nc.scalar.copy(
-                out=dst[:].rearrange("p (c i) t -> p c t i", i=4),
-                in_=state[c][h][:, :, cols].rearrange("p t (c i) -> p c t i", i=4),
-            )
-            grouped[(s, c, h, cols.start)] = dst
+        def group_state(s, c, h, e, n0=0, n1=None):
+            if (s, c, h) not in grouped:
+                grouped[(s, c, h)] = stage.tile([P, WIDTH[c], 4], BF16, name="half", align_bytes=256, bufs=8)
+            dst = grouped[(s, c, h)][:, n0:n1, :]
+            if e == "G":
+                copier[e](out=dst, in_=state[c][h][:, :, n0:n1].rearrange("p t n -> p n t"))
+            else:
+                copier[e](
+                    out=dst.rearrange("p (c i) t -> p c t i", i=4),
+                    in_=state[c][h][:, :, n0:n1].rearrange("p t (c i) -> p c t i", i=4),
+                )
 
-        def quantize_state(s, c, h, cols):
+        def quantize_state(s, c, h):
             cd, sc = codes_of(s + 1, c)
-            src = grouped[(s, c, h, cols.start)]
-            nc.vector.quantize_mx(out=cd[:, h, cols].bitcast(FP8X4), scales=sc[:, h, cols], in_=src[:].rearrange("p n t -> p (n t)"))
+            nc.vector.quantize_mx(out=cd[:, h, :].bitcast(FP8X4), scales=sc[:, h, :], in_=grouped[(s, c, h)][:].rearrange("p n t -> p (n t)"))
 
-        def turn_out(c, h, blocks, by_tile):
+        def turn_out(c, h, blocks, by_tile=False):
             for b in blocks:
                 turned[(c, h, b)] = take((c, h, b), [P, 4, P])
-            steps = [(b, t) for t in (1, 0, 3, 2) for b in blocks] if by_tile else [(b, t) for b in blocks for t in range(4)]
+            steps = [(b, t) for t in range(4) for b in blocks] if by_tile else [(b, t) for b in blocks for t in range(4)]
             for b, t in steps:
                 nc.tensor.transpose(turned[(c, h, b)][:, t, :], state[c][h][:, t, P * b : P * (b + 1)], ident[:])
 
-        def store(c, h, b, copy, queue):
+        def store(c, h, b, e, queue):
             res = stage.tile([P, 512], F32, name="res", bufs=8)
-            copy(out=res[:].rearrange("p (m t) -> p m t", t=4), in_=turned[(c, h, b)][:].rearrange("p t m -> p m t"))
+            copier[e](out=res[:].rearrange("p (m t) -> p m t", t=4), in_=turned[(c, h, b)][:].rearrange("p t m -> p m t"))
             give((c, h, b))
-            queue.dma_start(out=hbm_rows(out, c)[:, b, 512 * h : 512 * (h + 1)], in_=res[:])
+            queue.dma_start(out=hbm_rows(out, FIRST[c] + b // 2)[:, b % 2, 512 * h : 512 * (h + 1)], in_=res[:])
 
-        order = [(0, 0), (0, 1), (1, 0), (1, 1), (2, 0), (0, 2), (2, 1)]
-        units = [(0, 0, 0, cols) for cols in PAIRS] + [(s, c, h, WHOLE) for s, c in order for h in range(2)][1:]
-        units += [(s, LAST, h, cols) for s in (1, 2) for cols in PAIRS for h in range(2)]
+        def finish(c, h, blocks, engines="SSSS", by_tile=False):
+            turn_out(c, h, blocks, by_tile)
+            for b, e in zip(blocks, engines):
+                store(c, h, b, e, nc.scalar if by_tile and e == "S" else nc.sync)
 
-        def turn_q_pair(c, pair):
+        def warm(n):
+            bank = take("warm", [P, 512])
+            for t in range(n):
+                nc.tensor.matmul_mx(out=bank[:], lhsT=w_codes[:, 0, 0, 0:P].bitcast(FP8X4), lhsT_scale=w_scales[:, 0, 0, 0:P], rhs=w_codes[:, 0, 0, :].bitcast(FP8X4), rhs_scale=w_scales[:, 0, 0, :], start=True, stop=True)
+            give("warm")
+
+        def turn_pair(c, pair):
             for b in (2 * pair, 2 * pair + 1):
                 turn_q(c, b)
-            for b in (2 * pair + 1, 2 * pair):
+
+        def copy_pair(c, pair):
+            for b in (2 * pair, 2 * pair + 1):
                 copy_q(c, b)
 
-        def finish(c, h, blocks, share=False):
-            turn_out(c, h, blocks, share)
-            for b in blocks:
-                if share and b % 2:
-                    store(c, h, b, nc.vector.tensor_copy, nc.sync)
-                else:
-                    store(c, h, b, nc.scalar.copy, nc.scalar if share else nc.sync)
+        def store_some(c, h, blocks, engines="SSSS"):
+            for b, e in zip(blocks, engines):
+                store(c, h, b, e, nc.scalar if (c, h, e) == (LAST, 1, "S") else nc.sync)
 
-        group_w(0, 0, nc.vector.tensor_copy)
-        for b in range(2):
-            turn_q(0, b)
-            copy_q(0, b)
-        quantize_w(0, 0)
-        group_w(0, 1, nc.vector.tensor_copy)
-        for b in range(2, 4):
-            turn_q(0, b)
-            copy_q(0, b)
-        for g in range(2):
-            quantize_q(0, g, PAIRS[0])
-        quantize_w(0, 1)
-        group_w(1, 0, nc.vector.tensor_copy)
-        group_w(1, 1, nc.scalar.copy)
-        for g in range(2):
-            quantize_q(0, g, PAIRS[1])
-        nc.gpsimd.tensor_copy(out=inv[:], in_=inv16[:])
-        waiting = []
-        for i, (s, c, h, cols) in enumerate(units):
-            for k in range(4):
-                multiply(s, c, h, k, cols, 1 if i < 3 else 2)
-                if (i, k) in W_AT:
-                    quantize_w(1, W_AT.index((i, k)))
-                if (i, k) in TURN_Q_AT:
-                    n = TURN_Q_AT.index((i, k))
-                    turn_q_pair(1 + n // 2, n % 2)
-                if (i, k) in QUANT_Q_AT:
-                    quantize_q_whole(1 + QUANT_Q_AT.index((i, k)))
-                if (i, k) in FINISH_AT:
-                    finish(*FINISH_AT[(i, k)])
-                if k == 0 and not QUIET[0] <= i <= QUIET[1] or (i, k) == (QUIET[1], 3):
-                    for j in [j for j in waiting if j <= i - 2]:
-                        waiting.remove(j)
-                        quantize_state(*units[j][:3], WHOLE if j == 1 else units[j][3])
-            if s < 2 and i > 0:
-                group_state(s, c, h, WHOLE if i == 1 else cols)
-                waiting.append(i)
-        finish(LAST, 1, (2, 3), True)
+        def widen():
+            nc.gpsimd.tensor_copy(out=inv[:], in_=inv16[:])
+
+        do = {"gw": group_w, "qw": quantize_w, "tq": turn_q, "cq": copy_q, "tp": turn_q_pair, "qq": quantize_q, "gs": group_state,
+              "qs": quantize_state, "fin": finish, "sc": scale, "wid": widen, "warm": warm, "T": turn_pair, "C": copy_pair, "F": turn_out, "O": store_some}
+        for x in HEAD:
+            do[x[0]](*x[1:])
+        units = [(s, c, h) for s, c in ORDER for h in range(2)]
+        made = {(0, 0, 0), (0, 0, 1)}
+        w_made = {x[1:] for x in HEAD if x[0] == "qw"}
+        ready = set()
+
+        def may(x):
+            if x[0] == "M":
+                kind, i, t, gs = x
+                s, c, h = units[i]
+                return all((s, c, g) in made and any(y[:2] == (h, g) and (len(y) == 2 or y[2] <= t < y[3]) for y in w_made) for g in gs) and (0 not in gs or len(free) > 0 and (gs == (0,) or len(held) < LEAD))
+            if x[0] == "tp":
+                return len(free) >= 2
+            return len(free) >= len(x[3]) and (x[1], x[2], 3) in ready or x[-1] is True and (x[1], x[2], 3) in ready
+
+        tensor = []
+        for i in range(len(units)):
+            if i in SPLIT:
+                tensor.extend([("M", i, t, (0,)) for t in range(4)])
+            for t in range(4):
+                tensor.append(("M", i, t, (1,) if i in SPLIT else (0, 1)))
+                tensor.extend(AFTER_M.get((i, t), []))
+
+        late = []
+
+        def flush(n):
+            for y in list(late):
+                y[0] = y[0] - n
+                if y[0] <= 0:
+                    late.remove(y)
+                    do[y[1][0]](*y[1][1:])
+
+        def feed():
+            while tensor and may(tensor[0]):
+                x = tensor.pop(0)
+                if x[0] == "M":
+                    kind, i, t, gs = x
+                    s, c, h = units[i]
+                    if 0 in gs:
+                        held[(i, t)] = take(("m", i, t), [P, WIDTH[c]])
+                    for g in gs:
+                        one_pass(held[(i, t)], s, c, h, t, g)
+                elif x[0] == "tp":
+                    turn_pair(*x[1:])
+                    late.append([DELAY, ("C",) + x[1:]])
+                else:
+                    turn_out(x[1], x[2], x[3], x[-1] is True)
+                    if x[0] == "fin":
+                        late.append([DELAY, ("O",) + x[1:5]])
+
+        for i, (s, c, h) in enumerate(units):
+            for t in range(4):
+                feed()
+                advance(held.pop((i, t)), s, c, h, t)
+                give(("m", i, t))
+                if s == 2:
+                    ready.add((c, h, t))
+                flush(1)
+                for x in AFTER_A.get((i, t), []):
+                    if x[0] == "qq":
+                        flush(9)
+                    do[x[0]](*x[1:])
+                    if x[0] == "qs":
+                        made.add((x[1] + 1, x[2], x[3]))
+                    if x[0] == "qq":
+                        made.add((0, x[1], 0))
+                        made.add((0, x[1], 1))
+                    if x[0] == "qw":
+                        w_made.add(x[1:])
+                    feed()
+        while tensor or late:
+            feed()
+            flush(9)

@@ -21,22 +21,16 @@ CHUNKS = len(WIDTH)
 FIRST = [sum(WIDTH[:c]) // PAIR for c in range(CHUNKS)]
 LAST = CHUNKS - 1
 ORDER = [(0, 0), (0, 1), (1, 0), (1, 1), (2, 0), (0, 2), (2, 1), (1, 2), (0, 3), (2, 2), (1, 3), (2, 3)]
-AFTER_M = {(0,3):[("tp",1,1)],(1,3):[("tp",2,0)],(4,3):[("tp",2,1)],(7,1):[("tp",3,0)],(11,1):[("fin",0,0,(0,1))],(12,3):[("fin",0,1,(0,1))],(14,1):[("fin",1,0,(0,1))],(14,3):[("fin",1,0,(2,3))],(16,1):[("fin",1,1,(0,1))],(18,3):[("fin",1,1,(2,3))],(20,3):[("fin",2,0,(0,1))],(21,1):[("fin",2,0,(2,3))],(21,3):[("F",2,1,(0,1)),("F",2,1,(2,3))],(23,3):[("fin",3,0,(0,1),"SS"),("fin",3,1,(0,1),"SV",True)]}
-AFTER_A = {(0,1):[("qw",1,0,2,4)],(0,3):[("qw",1,1,2,4),("gs",0,0,0,"S")],(1,1):[("qq",1)],(1,3):[("qs",0,0,0),("gs",0,0,1,"S")],
-(2,3):[("qs",0,0,1),("gs",0,1,0,"S",0,256),("gs",0,1,0,"G",256,512)],(3,3):[("qs",0,1,0),("gs",0,1,1,"S",0,256),("gs",0,1,1,"G",256,512)],
-(4,3):[("gs",1,0,0,"S")],(5,3):[("qs",0,1,1),("gs",1,0,1,"S"),("qq",2),("qs",1,0,0)],
-(6,3):[("qs",1,0,1),("gs",1,1,0,"S",0,256),("gs",1,1,0,"G",256,512)],(7,3):[("qs",1,1,0),("gs",1,1,1,"S",0,256),("gs",1,1,1,"G",256,512)],
-(9,3):[("qq",3),("qs",1,1,1)],(10,3):[("gs",0,2,0,"S",0,256),("gs",0,2,0,"G",256,512)],(11,3):[("qs",0,2,0),("gs",0,2,1,"S",0,256),("gs",0,2,1,"G",256,512)],
-(12,3):[("qs",0,2,1)],(14,3):[("gs",1,2,0,"S",0,256),("gs",1,2,0,"G",256,512)],(15,3):[("qs",1,2,0),("gs",1,2,1,"S",0,256),("gs",1,2,1,"G",256,512)],
-(16,3):[("gs",0,3,0,"S")],(17,3):[("qs",1,2,1),("gs",0,3,1,"S"),("qs",0,3,0)],(18,3):[("qs",0,3,1)],
-(20,3):[("gs",1,3,0,"S"),("sc",3,0,"G",0,2),("sc",3,0,"S",2,4)],(21,3):[("qs",1,3,0),("gs",1,3,1,"V"),("sc",3,1,"V",0,2),("qs",1,3,1),("sc",3,1,"V",2,4),("O",2,1,(0,1),"SS"),("O",2,1,(2,3),"SS")]}
+AFTER_M = {(0,3):[("tp",1,1)],(1,3):[("tp",2,0)],(3,3):[("tp",2,1)],(7,1):[("tp",3,0)],(11,2):[("fin",0,0,(0,1))],(13,1):[("fin",0,1,(0,1))],(14,2):[("fin",1,0,(0,1))],(15,3):[("fin",1,0,(2,3))],(17,3):[("fin",1,1,(0,1))],(18,2):[("fin",1,1,(2,3))],(19,3):[("fin",2,0,(0,1))],(21,3):[("F",2,0,(2,3)),("F",2,1,(0,1))],(22,-1):[("F",2,1,(2,3))],(23,3):[("F",3,0,(0,1)),("F",3,1,(0,1),True)]}
+AFTER_A = {(2,0):[("sort",2,1,"S")],(0,1):[("qw",1,0,2,4)],(0,3):[("qw",1,1,2,4),("gs",0,0,0,"S")],(1,3):[("qs",0,0,0),("gs",0,0,1,"S")],(2,3):[("qs",0,0,1),("gs",0,1,0,"S",0,256),("gs",0,1,0,"G",256,512)],(3,3):[("qs",0,1,0),("gs",0,1,1,"S",0,256),("gs",0,1,1,"G",256,512)],(5,1):[("qs",0,1,1)],(5,3):[("sort",3,0,"S"),("qs",1,0,0),("qq",2),("gs",1,0,1,"S")],(6,3):[("qs",1,0,1),("gs",1,1,0,"S",0,256),("gs",1,1,0,"G",256,512)],(7,3):[("qs",1,1,0),("gs",1,1,1,"S",0,256),("gs",1,1,1,"G",256,512)],(10,3):[("qs",1,1,1),("gs",0,2,0,"S",0,256),("gs",0,2,0,"G",256,512)],(11,3):[("qs",0,2,0),("gs",0,2,1,"S",0,256),("gs",0,2,1,"G",256,512)],(12,3):[("qs",0,2,1),("qq",3)],(15,3):[("qs",1,2,0),("gs",1,2,1,"S",0,256),("gs",1,2,1,"G",256,512)],(17,1):[("qs",1,2,1)],(17,3):[("qs",0,3,0),("gs",0,3,1,"S")],(18,3):[("qs",0,3,1)],(1,1):[("qq",1)],(4,3):[("gs",1,0,0,"S")],(14,3):[("gs",1,2,0,"S",0,256),("gs",1,2,0,"G",256,512)],(16,3):[("gs",0,3,0,"S")],(20,3):[("gs",1,3,0,"S"),("sc",3,0,"G",0,3)],(21,3):[("qs",1,3,0),("gs",1,3,1,"V"),("sc",3,0,"V",3,4),("O",2,0,(2,3),"SS"),("qs",1,3,1),("sc",3,1,"V"),("O",2,1,(0,1),"SS"),("O",2,1,(2,3),"SS")],(23,3):[("O",3,0,(0,1),"SV"),("O",3,1,(0,1),"SV")]}
 SPLIT = (0, 6, 18, 22)
-DELAY = 3
-LEAD = 3
-ON_G = (0, 1)
+PACKED = (8, 9)
+DELAY = 4
+LEAD = 4
+ON_G = (3,)
 VIA_S = ()
-LOADS = [(0, 0), (0,), (0, 1), (1, 0), (1,), (1, 1), (2,), (3,), (4,), (5,)]
-HEAD = [("gw",0,0,"V",0,2),("gw",0,0,"S",2,4),("tq",0,0),("cq",0,0),("tq",0,1),("cq",0,1),("qw",0,0),("gw",0,1,"V"),("gw",1,0,"V",0,2),("qq",0),("qw",0,1),("gw",1,0,"S",2,4),("gw",1,1,"S",2,4),("T",1,0),("C",1,0),("gw",1,1,"V",0,2),("qw",1,0,0,2),("qw",1,1,0,2),("wid",)]
+LOADS = [(0, 0), (0,), (1,), (0, 1), (1, 0), (1, 1), (2,), (3,), (4,), (5,)]
+HEAD = [("gw",0,0,"V",0,2),("gw",0,0,"S",2,4),("tq",0,0),("cq",0,0),("tq",0,1),("cq",0,1),("T",1,0),("C",1,0),("qw",0,0),("gw",0,1,"V"),("qq",0),("qw",0,1),("gw",1,0,"V",0,2),("gw",1,0,"S",2,4),("gw",1,1,"S",2,4),("gw",1,1,"V",0,2),("qw",1,0,0,2),("qw",1,1,0,2),("wid",)]
 TAIL = []
 EARLY_SCALE = [3]
 
@@ -137,12 +131,25 @@ def tile_dense_heat_steps_t1_kernel(tc, q, w, heater, inv_cap, out):
                 in_=w_grouped[(h, g)][:, 512 * t0 : 512 * t1],
             )
 
+        sorted_q = {}
+
+        def sort_q(c, pair, e):
+            j = FIRST[c] + pair
+            dst = stage.tile([P, 2, 512], F32, name="sorted", bufs=2)
+            copier[e](
+                out=dst[:].rearrange("p b (g u m) -> p (b g) u m", g=2, u=2),
+                in_=q_rows[j][:].rearrange("p b k -> p (b k)").bitcast(F32).rearrange("p (a m u) -> p a u m", a=4, u=2),
+            )
+            sorted_q[j] = dst
+
         def turn_q(c, b):
             words = q_rows[FIRST[c] + b // 2][:, b % 2, :].bitcast(F32)
             bank = take((c, b), [P, 4, P])
             for g in range(2):
                 for u in range(2):
-                    nc.tensor.transpose(bank[:, 2 * g + u, :], words[:, 256 * g + u : 256 * (g + 1) : 2], ident[:])
+                    j = FIRST[c] + b // 2
+                    src = sorted_q[j][:, b % 2, P * (2 * g + u) : P * (2 * g + u + 1)] if j in sorted_q else words[:, 256 * g + u : 256 * (g + 1) : 2]
+                    nc.tensor.transpose(bank[:, 2 * g + u, :], src, ident[:])
             turned[(c, b)] = bank
 
         def copy_q(c, b, e="S"):
@@ -168,7 +175,7 @@ def tile_dense_heat_steps_t1_kernel(tc, q, w, heater, inv_cap, out):
             cd, sc = codes_of(s, c)
             cells = slice(P * t, P * (t + 1))
             nc.tensor.matmul_mx(
-                out=bank[:],
+                out=bank,
                 lhsT=w_codes[:, h, g, cells].bitcast(FP8X4),
                 lhsT_scale=w_scales[:, h, g, cells],
                 rhs=cd[:, g, :].bitcast(FP8X4),
@@ -194,23 +201,26 @@ def tile_dense_heat_steps_t1_kernel(tc, q, w, heater, inv_cap, out):
             if (s, c, h, t) in VIA_S:
                 part = stage.tile([P, WIDTH[c]], F32, name="part", bufs=2)
                 if s < 2:
-                    nc.scalar.activation(part[:], bank[:], mybir.ActivationFunctionType.Identity, bias=heat[:, h, t : t + 1])
+                    nc.scalar.activation(part[:], bank, mybir.ActivationFunctionType.Identity, bias=heat[:, h, t : t + 1])
                 else:
-                    nc.scalar.copy(part[:], bank[:])
+                    nc.scalar.copy(part[:], bank)
                 nc.gpsimd.tensor_tensor(now, part[:], q_words[c][:, h, :, t] if s == 0 else now, ADD)
                 if s == 2:
                     nc.gpsimd.tensor_scalar(now, now, inv[:, h, t : t + 1], 0.0, MULT, ADD)
             elif s == 0:
-                nc.vector.scalar_tensor_tensor(now, bank[:], heat[:, h, t : t + 1], q_words[c][:, h, :, t], ADD, ADD)
+                nc.vector.scalar_tensor_tensor(now, bank, heat[:, h, t : t + 1], q_words[c][:, h, :, t], ADD, ADD)
             elif s == 1:
-                nc.vector.scalar_tensor_tensor(now, bank[:], heat[:, h, t : t + 1], now, ADD, ADD)
+                nc.vector.scalar_tensor_tensor(now, bank, heat[:, h, t : t + 1], now, ADD, ADD)
             elif c in EARLY_SCALE:
-                nc.vector.scalar_tensor_tensor(now, bank[:], inv[:, h, t : t + 1], scaled[(c, h)][:, t, :], MULT, ADD)
+                nc.vector.scalar_tensor_tensor(now, bank, inv[:, h, t : t + 1], scaled[(c, h)][:, t, :], MULT, ADD)
             else:
-                nc.vector.tensor_tensor(now, bank[:], now, ADD)
-                if t in ON_G:
+                nc.vector.tensor_tensor(now, bank, now, ADD)
+                if h == 1 and t < 2:
                     nc.gpsimd.tensor_scalar(now, now, inv[:, h, t : t + 1], 0.0, MULT, ADD)
-                else:
+                elif h == 0 and t == 3:
+                    for u in ON_G:
+                        nc.gpsimd.tensor_scalar(state[c][h][:, u, :], state[c][h][:, u, :], inv[:, h, u : u + 1], 0.0, MULT, ADD)
+                elif h == 1 or t not in ON_G:
                     nc.scalar.mul(now, now, inv[:, h, t : t + 1])
 
         def scale(c, h, e, t0=0, t1=4):
@@ -278,7 +288,7 @@ def tile_dense_heat_steps_t1_kernel(tc, q, w, heater, inv_cap, out):
             nc.gpsimd.tensor_copy(out=inv[:], in_=inv16[:])
 
         do = {"gw": group_w, "qw": quantize_w, "tq": turn_q, "cq": copy_q, "tp": turn_q_pair, "qq": quantize_q, "gs": group_state,
-              "qs": quantize_state, "fin": finish, "sc": scale, "wid": widen, "warm": warm, "T": turn_pair, "C": copy_pair, "F": turn_out, "O": store_some}
+              "qs": quantize_state, "fin": finish, "sc": scale, "wid": widen, "sort": sort_q, "warm": warm, "T": turn_pair, "C": copy_pair, "F": turn_out, "O": store_some}
         for x in HEAD:
             do[x[0]](*x[1:])
         units = [(s, c, h) for s, c in ORDER for h in range(2)]
@@ -290,20 +300,22 @@ def tile_dense_heat_steps_t1_kernel(tc, q, w, heater, inv_cap, out):
             if x[0] == "M":
                 kind, i, t, gs = x
                 s, c, h = units[i]
-                return all((s, c, g) in made and any(y[:2] == (h, g) and (len(y) == 2 or y[2] <= t < y[3]) for y in w_made) for g in gs) and (0 not in gs or len(free) > 0 and (gs == (0,) or len(held) < LEAD))
+                return all((s, c, g) in made and any(y[:2] == (h, g) and (len(y) == 2 or y[2] <= t < y[3]) for y in w_made) for g in gs) and (0 not in gs or i in PACKED and t % 2 or len(free) > 0 and (gs == (0,) or len([k for k in number if k[0] == "m"]) < LEAD))
             if x[0] == "tp":
-                return len(free) >= 2
+                return len(free) >= 2 and (FIRST[x[1]] + x[2] in sorted_q or FIRST[x[1]] + x[2] < 4)
             return len(free) >= len(x[3]) and (x[1], x[2], 3) in ready or x[-1] is True and (x[1], x[2], 3) in ready
 
         tensor = []
         for i in range(len(units)):
             if i in SPLIT:
                 tensor.extend([("M", i, t, (0,)) for t in range(4)])
+                tensor.extend(AFTER_M.get((i, -1), []))
             for t in range(4):
                 tensor.append(("M", i, t, (1,) if i in SPLIT else (0, 1)))
                 tensor.extend(AFTER_M.get((i, t), []))
 
         late = []
+        both = {}
 
         def flush(n):
             for y in list(late):
@@ -318,8 +330,15 @@ def tile_dense_heat_steps_t1_kernel(tc, q, w, heater, inv_cap, out):
                 if x[0] == "M":
                     kind, i, t, gs = x
                     s, c, h = units[i]
-                    if 0 in gs:
-                        held[(i, t)] = take(("m", i, t), [P, WIDTH[c]])
+                    packed = i in PACKED
+                    if packed and t % 2:
+                        held[(i, t)] = both[i][:, 1, :]
+                    elif packed:
+                        both[i] = take(("m", i, t + 1), [P, 2, PAIR])
+                        held[(i, t)] = both[i][:, 0, :]
+                    elif 0 in gs:
+                        bank = take(("m", i, t), [P, WIDTH[c]])
+                        held[(i, t)] = bank[:]
                     for g in gs:
                         one_pass(held[(i, t)], s, c, h, t, g)
                 elif x[0] == "tp":
@@ -334,10 +353,13 @@ def tile_dense_heat_steps_t1_kernel(tc, q, w, heater, inv_cap, out):
             for t in range(4):
                 feed()
                 advance(held.pop((i, t)), s, c, h, t)
-                give(("m", i, t))
+                if ("m", i, t) in number:
+                    give(("m", i, t))
                 if s == 2:
                     ready.add((c, h, t))
                 flush(1)
+                if i == len(units) - 1:
+                    feed()
                 for x in AFTER_A.get((i, t), []):
                     if x[0] == "qq":
                         flush(9)

@@ -13,33 +13,28 @@ U8 = mybir.dt.uint8
 FP8X4 = mybir.dt.float8_e4m3fn_x4
 ADD = mybir.AluOpType.add
 MULT = mybir.AluOpType.mult
+IDENTITY = mybir.ActivationFunctionType.Identity
 
 P = 128
-PAIR = 256
-WIDTH = [256, 512, 512, 256]
-CHUNKS = len(WIDTH)
-FIRST = [sum(WIDTH[:c]) // PAIR for c in range(CHUNKS)]
-LAST = CHUNKS - 1
+PAIR = 2 * P
+WIDE = 512
+UNIT = 4 * WIDE
+WIDTH = [PAIR, WIDE, WIDE, PAIR]
+FIRST = [sum(WIDTH[:c]) // PAIR for c in range(len(WIDTH))]
+LAST = len(WIDTH) - 1
 ORDER = [(0, 0), (0, 1), (1, 0), (1, 1), (2, 0), (0, 2), (2, 1), (1, 2), (0, 3), (2, 2), (1, 3), (2, 3)]
-AFTER_M = {(0,3):[("tp",1,1)],(1,3):[("tp",2,0)],(3,3):[("tp",2,1)],(7,1):[("tp",3,0)],(11,2):[("fin",0,0,(0,1))],(13,1):[("fin",0,1,(0,1))],(14,2):[("fin",1,0,(0,1))],(15,3):[("fin",1,0,(2,3))],(17,3):[("fin",1,1,(0,1))],(18,2):[("fin",1,1,(2,3))],(19,3):[("fin",2,0,(0,1))],(21,3):[("F",2,0,(2,3)),("F",2,1,(0,1))],(22,-1):[("F",2,1,(2,3))],(23,3):[("F",3,0,(0,1)),("F",3,1,(0,1),True)]}
-AFTER_A = {(2,0):[("sort",2,1,"S")],(0,1):[("qw",1,0,2,4)],(0,3):[("qw",1,1,2,4),("gs",0,0,0,"S")],(1,3):[("qs",0,0,0),("gs",0,0,1,"S")],(2,3):[("qs",0,0,1),("gs",0,1,0,"S",0,256),("gs",0,1,0,"G",256,512)],(3,3):[("qs",0,1,0),("gs",0,1,1,"S",0,256),("gs",0,1,1,"G",256,512)],(5,1):[("qs",0,1,1)],(5,3):[("sort",3,0,"S"),("qs",1,0,0),("qq",2),("gs",1,0,1,"S")],(6,3):[("qs",1,0,1),("gs",1,1,0,"S",0,256),("gs",1,1,0,"G",256,512)],(7,3):[("qs",1,1,0),("gs",1,1,1,"S",0,256),("gs",1,1,1,"G",256,512)],(10,3):[("qs",1,1,1),("gs",0,2,0,"S",0,256),("gs",0,2,0,"G",256,512)],(11,3):[("qs",0,2,0),("gs",0,2,1,"S",0,256),("gs",0,2,1,"G",256,512)],(12,3):[("qs",0,2,1),("qq",3)],(15,3):[("qs",1,2,0),("gs",1,2,1,"S",0,256),("gs",1,2,1,"G",256,512)],(17,1):[("qs",1,2,1)],(17,3):[("qs",0,3,0),("gs",0,3,1,"S")],(18,3):[("qs",0,3,1)],(1,1):[("qq",1)],(4,3):[("gs",1,0,0,"S")],(14,3):[("gs",1,2,0,"S",0,256),("gs",1,2,0,"G",256,512)],(16,3):[("gs",0,3,0,"S")],(20,3):[("gs",1,3,0,"S"),("sc",3,0,"G",0,3)],(21,3):[("qs",1,3,0),("gs",1,3,1,"V"),("sc",3,0,"V",3,4),("O",2,0,(2,3),"SS"),("qs",1,3,1),("sc",3,1,"V"),("O",2,1,(0,1),"SS"),("O",2,1,(2,3),"SS")],(23,3):[("O",3,0,(0,1),"SV"),("O",3,1,(0,1),"SV")]}
-SPLIT = (0, 6, 18, 22)
-PACKED = (8, 9)
-DELAY = 4
 LEAD = 4
-ON_G = (3,)
-VIA_S = ()
-LOADS = [(0, 0), (0,), (1,), (0, 1), (1, 0), (1, 1), (2,), (3,), (4,), (5,)]
-HEAD = [("gw",0,0,"V",0,2),("gw",0,0,"S",2,4),("tq",0,0),("cq",0,0),("tq",0,1),("cq",0,1),("T",1,0),("C",1,0),("qw",0,0),("gw",0,1,"V"),("qq",0),("qw",0,1),("gw",1,0,"V",0,2),("gw",1,0,"S",2,4),("gw",1,1,"S",2,4),("gw",1,1,"V",0,2),("qw",1,0,0,2),("qw",1,1,0,2),("wid",)]
-TAIL = []
-EARLY_SCALE = [3]
+AHEAD = 2
+SPACING = 2048
+SHARE = 256
+ON_GPSIMD = 2
 
 
 def tile_dense_heat_steps_t1_kernel(tc, q, w, heater, inv_cap, out):
     nc = tc.nc
     with ExitStack() as ctx:
         keep = ctx.enter_context(tc.tile_pool(name="keep", bufs=1))
-        stage = ctx.enter_context(tc.tile_pool(name="stage", bufs=4))
+        stage = ctx.enter_context(tc.tile_pool(name="stage", bufs=8))
         psum = ctx.enter_context(tc.psum_pool(name="psum", bufs=1))
         ctx.enter_context(tc.manual_schedule())
 
@@ -49,58 +44,33 @@ def tile_dense_heat_steps_t1_kernel(tc, q, w, heater, inv_cap, out):
         inv = keep.tile([P, 2, 4], F32, name="inv")
         w_codes = keep.tile([P, 2, 2, 512], U32, name="w_codes", align_bytes=256)
         w_scales = keep.tile([P, 2, 2, 512], U8, name="w_scales", align_bytes=256)
-        q_words = [keep.tile([P, 2, WIDTH[c], 4], BF16, name="q_words%d" % c, align_bytes=256) for c in range(CHUNKS)]
-        state = [[keep.tile([P, 4, WIDTH[c]], F32, name="state%d%d" % (c, h)) for h in range(2)] for c in range(CHUNKS)]
-        scaled = {(c, h): keep.tile([P, 4, WIDTH[c]], F32, name="scaled%d%d" % (c, h)) for h in range(2) for c in EARLY_SCALE}
+        q_words = [keep.tile([P, 2, n, 4], BF16, name="q_words%d" % c, align_bytes=256) for c, n in enumerate(WIDTH)]
+        state = [[keep.tile([P, 4, n], F32, name="state%d%d" % (c, h)) for h in range(2)] for c, n in enumerate(WIDTH)]
+        scaled = [keep.tile([P, 4, WIDTH[LAST]], F32, name="scaled%d" % h) for h in range(2)]
+
+        q_rows, w_rows, w_grouped, grouped, codes, turned, held = {}, {}, {}, {}, {}, {}, {}
+        free, spare, number = list(range(LEAD)), list(range(LEAD, 8)), {}
+
+        def take(key, shape, lent=False):
+            number[key] = free.pop(0) if key[0] == "pass" or lent else spare.pop(0)
+            bank = psum.tile(shape, F32, name="bank%d" % number[key])
+            return bank
+
+        def give(key):
+            n = number.pop(key)
+            (free if n < LEAD else spare).append(n)
 
         def hbm_rows(x, j):
             return x[PAIR * j : PAIR * (j + 1), :].rearrange("(p b) k -> p b k", b=2)
 
-        q_rows = {}
-        w_rows = {}
-
         def load_q(j):
-            rows = keep.tile([P, 2, N], BF16, name="q_rows%d" % j, align_bytes=256)
-            nc.sync.dma_start(out=rows[:], in_=hbm_rows(q, j))
-            q_rows[j] = rows
+            q_rows[j] = keep.tile([P, 2, N], BF16, name="q_rows%d" % j, align_bytes=256)
+            nc.sync.dma_start(out=q_rows[j][:], in_=hbm_rows(q, j))
 
         def load_w(h, g):
-            rows = stage.tile([P, 4, 512], BF16, name="half", align_bytes=256, bufs=8)
+            w_rows[(h, g)] = stage.tile([P, 4, 512], BF16, name="half", align_bytes=256)
             src = w[512 * g : 512 * (g + 1), 512 * h : 512 * (h + 1)].rearrange("(p j) c -> p j c", j=4)
-            nc.sync.dma_start(out=rows[:], in_=src)
-            w_rows[(h, g)] = rows
-
-        make_identity(nc, ident[:])
-        nc.scalar.dma_start(out=heat[:], in_=heater.rearrange("(g p t) -> p g t", g=2, t=4))
-        for x in LOADS:
-            if len(x) == 1:
-                load_q(*x)
-            else:
-                load_w(*x)
-        nc.sync.dma_start(out=inv16[:], in_=inv_cap.rearrange("(g p t) -> p g t", g=2, t=4))
-
-        codes = {}
-        held = {}
-        free = list(range(8))
-        number = {}
-
-        def take(key, shape):
-            n = free.pop(0)
-            number[key] = n
-            bank = psum.tile(shape, F32, name="bank%d" % n)
-            return bank
-
-        def give(key):
-            free.append(number.pop(key))
-
-        turned = {}
-        grouped = {}
-        w_grouped = {}
-
-        def on_gpsimd(out, in_):
-            nc.gpsimd.tensor_scalar(out, in_, 1.0, 0.0, MULT, ADD)
-
-        copier = {"V": nc.vector.tensor_copy, "S": nc.scalar.copy, "G": on_gpsimd}
+            nc.sync.dma_start(out=w_rows[(h, g)][:], in_=src)
 
         def codes_of(s, c):
             if (s, c) not in codes:
@@ -109,59 +79,33 @@ def tile_dense_heat_steps_t1_kernel(tc, q, w, heater, inv_cap, out):
                 codes[(s, c)] = (cd, sc)
             return codes[(s, c)]
 
-        def group_w(h, g, e, t0=0, t1=4):
+        def group_w(h, g, copy, t0, t1):
             if (h, g) not in w_grouped:
-                w_grouped[(h, g)] = stage.tile([P, 2048], BF16, name="half", align_bytes=256, bufs=8)
-            dst = w_grouped[(h, g)]
-            if e == "G":
-                copier[e](
-                    out=dst[:].rearrange("p (t m j) -> p t m j", t=4, j=4)[:, t0:t1],
-                    in_=w_rows[(h, g)][:].rearrange("p j (m t) -> p t m j", t=4)[:, t0:t1],
-                )
-            else:
-                copier[e](
-                    out=dst[:].rearrange("p (t m i j) -> p m t i j", t=4, i=2, j=4)[:, :, t0:t1],
-                    in_=w_rows[(h, g)][:].rearrange("p j (m i t) -> p m t i j", t=4, i=2)[:, :, t0:t1],
-                )
+                w_grouped[(h, g)] = stage.tile([P, 2048], BF16, name="half", align_bytes=256)
+            copy(
+                out=w_grouped[(h, g)][:].rearrange("p (t m i j) -> p m t i j", t=4, i=2, j=4)[:, :, t0:t1],
+                in_=w_rows[(h, g)][:].rearrange("p j (m i t) -> p m t i j", t=4, i=2)[:, :, t0:t1],
+            )
 
-        def quantize_w(h, g, t0=0, t1=4):
+        def quantize_w(h, g, t0, t1):
             nc.vector.quantize_mx(
                 out=w_codes[:, h, g, P * t0 : P * t1].bitcast(FP8X4),
                 scales=w_scales[:, h, g, P * t0 : P * t1],
                 in_=w_grouped[(h, g)][:, 512 * t0 : 512 * t1],
             )
 
-        sorted_q = {}
-
-        def sort_q(c, pair, e):
-            j = FIRST[c] + pair
-            dst = stage.tile([P, 2, 512], F32, name="sorted", bufs=2)
-            copier[e](
-                out=dst[:].rearrange("p b (g u m) -> p (b g) u m", g=2, u=2),
-                in_=q_rows[j][:].rearrange("p b k -> p (b k)").bitcast(F32).rearrange("p (a m u) -> p a u m", a=4, u=2),
-            )
-            sorted_q[j] = dst
-
         def turn_q(c, b):
             words = q_rows[FIRST[c] + b // 2][:, b % 2, :].bitcast(F32)
-            bank = take((c, b), [P, 4, P])
+            turned[("q", c, b)] = take(("q", c, b), [P, 4, P])
             for g in range(2):
                 for u in range(2):
-                    j = FIRST[c] + b // 2
-                    src = sorted_q[j][:, b % 2, P * (2 * g + u) : P * (2 * g + u + 1)] if j in sorted_q else words[:, 256 * g + u : 256 * (g + 1) : 2]
-                    nc.tensor.transpose(bank[:, 2 * g + u, :], src, ident[:])
-            turned[(c, b)] = bank
+                    nc.tensor.transpose(turned[("q", c, b)][:, 2 * g + u, :], words[:, 256 * g + u : 256 * (g + 1) : 2], ident[:])
 
-        def copy_q(c, b, e="S"):
+        def copy_q(c, b):
             dst = q_words[c][:, :, P * b : P * (b + 1), :].rearrange("p g n t -> p g (n t)").bitcast(F32)
-            copier[e](out=dst.rearrange("p g (n u) -> p g n u", u=2), in_=turned[(c, b)][:].rearrange("p (g u) n -> p g n u", g=2))
-            give((c, b))
-
-        def turn_q_pair(c, pair):
-            for b in (2 * pair, 2 * pair + 1):
-                turn_q(c, b)
-            for b in (2 * pair, 2 * pair + 1):
-                copy_q(c, b)
+            src = turned[("q", c, b)][:].rearrange("p (g u) n -> p g n u", g=2)
+            nc.scalar.copy(out=dst.rearrange("p g (n u) -> p g n u", u=2), in_=src)
+            give(("q", c, b))
 
         def quantize_q(c):
             cd, sc = codes_of(0, c)
@@ -184,194 +128,218 @@ def tile_dense_heat_steps_t1_kernel(tc, q, w, heater, inv_cap, out):
                 stop=(g == 1),
             )
 
-        def multiply(s, c, h, t, split):
-            if split and t == 0:
-                for u in range(4):
-                    held[u] = take(u, [P, WIDTH[c]])
-                    one_pass(held[u], s, c, h, u, 0)
-            if not split:
-                held[t] = take(t, [P, WIDTH[c]])
-                one_pass(held[t], s, c, h, t, 0)
-            one_pass(held[t], s, c, h, t, 1)
-            advance(held[t], s, c, h, t)
-            give(t)
-
-        def advance(bank, s, c, h, t):
+        def add_on_vector(bank, s, c, h, t):
             now = state[c][h][:, t, :]
-            if (s, c, h, t) in VIA_S:
-                part = stage.tile([P, WIDTH[c]], F32, name="part", bufs=2)
-                if s < 2:
-                    nc.scalar.activation(part[:], bank, mybir.ActivationFunctionType.Identity, bias=heat[:, h, t : t + 1])
-                else:
-                    nc.scalar.copy(part[:], bank)
-                nc.gpsimd.tensor_tensor(now, part[:], q_words[c][:, h, :, t] if s == 0 else now, ADD)
-                if s == 2:
-                    nc.gpsimd.tensor_scalar(now, now, inv[:, h, t : t + 1], 0.0, MULT, ADD)
-            elif s == 0:
+            if s == 0:
                 nc.vector.scalar_tensor_tensor(now, bank, heat[:, h, t : t + 1], q_words[c][:, h, :, t], ADD, ADD)
             elif s == 1:
                 nc.vector.scalar_tensor_tensor(now, bank, heat[:, h, t : t + 1], now, ADD, ADD)
-            elif c in EARLY_SCALE:
-                nc.vector.scalar_tensor_tensor(now, bank, inv[:, h, t : t + 1], scaled[(c, h)][:, t, :], MULT, ADD)
+            elif c == LAST:
+                nc.vector.scalar_tensor_tensor(now, bank, inv[:, h, t : t + 1], scaled[h][:, t, :], MULT, ADD)
             else:
                 nc.vector.tensor_tensor(now, bank, now, ADD)
-                if h == 1 and t < 2:
-                    nc.gpsimd.tensor_scalar(now, now, inv[:, h, t : t + 1], 0.0, MULT, ADD)
-                elif h == 0 and t == 3:
-                    for u in ON_G:
-                        nc.gpsimd.tensor_scalar(state[c][h][:, u, :], state[c][h][:, u, :], inv[:, h, u : u + 1], 0.0, MULT, ADD)
-                elif h == 1 or t not in ON_G:
-                    nc.scalar.mul(now, now, inv[:, h, t : t + 1])
 
-        def scale(c, h, e, t0=0, t1=4):
-            for t in range(t0, t1):
-                if e == "S":
-                    nc.scalar.mul(scaled[(c, h)][:, t, :], state[c][h][:, t, :], inv[:, h, t : t + 1])
-                elif e == "V":
-                    nc.vector.tensor_scalar(scaled[(c, h)][:, t, :], state[c][h][:, t, :], inv[:, h, t : t + 1], 0.0, MULT, ADD)
-                else:
-                    nc.gpsimd.tensor_scalar(scaled[(c, h)][:, t, :], state[c][h][:, t, :], inv[:, h, t : t + 1], 0.0, MULT, ADD)
+        def add_on_others(bank, s, c, h, t):
+            now = state[c][h][:, t, :]
+            part = stage.tile([P, WIDE], F32, name="part", bufs=2)
+            nc.scalar.activation(part[:], bank, IDENTITY, bias=heat[:, h, t : t + 1])
+            nc.gpsimd.tensor_tensor(now, part[:], q_words[c][:, h, :, t] if s == 0 else now, ADD)
 
-        def group_state(s, c, h, e, n0=0, n1=None):
-            if (s, c, h) not in grouped:
-                grouped[(s, c, h)] = stage.tile([P, WIDTH[c], 4], BF16, name="half", align_bytes=256, bufs=8)
-            dst = grouped[(s, c, h)][:, n0:n1, :]
-            if e == "G":
-                copier[e](out=dst, in_=state[c][h][:, :, n0:n1].rearrange("p t n -> p n t"))
-            else:
-                copier[e](
-                    out=dst.rearrange("p (c i) t -> p c t i", i=4),
-                    in_=state[c][h][:, :, n0:n1].rearrange("p t (c i) -> p c t i", i=4),
-                )
+        def scale(engine, dst, c, h, t):
+            engine.tensor_scalar(dst[:, t, :], state[c][h][:, t, :], inv[:, h, t : t + 1], 0.0, MULT, ADD)
+
+        def group_state(s, c, h, copy):
+            dst = stage.tile([P, WIDTH[c], 4], BF16, name="half", align_bytes=256)
+            grouped[(s, c, h)] = dst
+            n = min(SHARE, WIDTH[c])
+            copy(
+                out=dst[:, :n, :].rearrange("p (c i) t -> p c t i", i=4),
+                in_=state[c][h][:, :, :n].rearrange("p t (c i) -> p c t i", i=4),
+            )
+            if n < WIDTH[c]:
+                nc.gpsimd.tensor_scalar(dst[:, n:, :], state[c][h][:, :, n:].rearrange("p t n -> p n t"), 1.0, 0.0, MULT, ADD)
 
         def quantize_state(s, c, h):
             cd, sc = codes_of(s + 1, c)
-            nc.vector.quantize_mx(out=cd[:, h, :].bitcast(FP8X4), scales=sc[:, h, :], in_=grouped[(s, c, h)][:].rearrange("p n t -> p (n t)"))
+            src = grouped[(s, c, h)][:].rearrange("p n t -> p (n t)")
+            nc.vector.quantize_mx(out=cd[:, h, :].bitcast(FP8X4), scales=sc[:, h, :], in_=src)
 
-        def turn_out(c, h, blocks, by_tile=False):
+        def turn_out(c, h, pair, lent):
+            blocks = (2 * pair, 2 * pair + 1)
             for b in blocks:
-                turned[(c, h, b)] = take((c, h, b), [P, 4, P])
-            steps = [(b, t) for t in range(4) for b in blocks] if by_tile else [(b, t) for b in blocks for t in range(4)]
-            for b, t in steps:
+                turned[(c, h, b)] = take((c, h, b), [P, 4, P], lent)
+            by_block = [(b, t) for b in blocks for t in range(4)]
+            by_tile = [(b, t) for t in range(4) for b in blocks]
+            for b, t in by_tile if (c, h) == (LAST, 1) else by_block:
                 nc.tensor.transpose(turned[(c, h, b)][:, t, :], state[c][h][:, t, P * b : P * (b + 1)], ident[:])
 
-        def store(c, h, b, e, queue):
-            res = stage.tile([P, 512], F32, name="res", bufs=8)
-            copier[e](out=res[:].rearrange("p (m t) -> p m t", t=4), in_=turned[(c, h, b)][:].rearrange("p t m -> p m t"))
-            give((c, h, b))
-            queue.dma_start(out=hbm_rows(out, FIRST[c] + b // 2)[:, b % 2, 512 * h : 512 * (h + 1)], in_=res[:])
-
-        def finish(c, h, blocks, engines="SSSS", by_tile=False):
-            turn_out(c, h, blocks, by_tile)
-            for b, e in zip(blocks, engines):
-                store(c, h, b, e, nc.scalar if by_tile and e == "S" else nc.sync)
-
-        def warm(n):
-            bank = take("warm", [P, 512])
-            for t in range(n):
-                nc.tensor.matmul_mx(out=bank[:], lhsT=w_codes[:, 0, 0, 0:P].bitcast(FP8X4), lhsT_scale=w_scales[:, 0, 0, 0:P], rhs=w_codes[:, 0, 0, :].bitcast(FP8X4), rhs_scale=w_scales[:, 0, 0, :], start=True, stop=True)
-            give("warm")
-
-        def turn_pair(c, pair):
+        def store(c, h, pair, shared):
             for b in (2 * pair, 2 * pair + 1):
-                turn_q(c, b)
+                copy = nc.vector.tensor_copy if shared and b % 2 else nc.scalar.copy
+                queue = nc.scalar if (c, h, b) == (LAST, 1, 0) else nc.sync
+                res = stage.tile([P, 512], F32, name="res")
+                copy(out=res[:].rearrange("p (m t) -> p m t", t=4), in_=turned[(c, h, b)][:].rearrange("p t m -> p m t"))
+                give((c, h, b))
+                queue.dma_start(out=hbm_rows(out, FIRST[c] + pair)[:, b % 2, 512 * h : 512 * (h + 1)], in_=res[:])
 
-        def copy_pair(c, pair):
-            for b in (2 * pair, 2 * pair + 1):
-                copy_q(c, b)
+        make_identity(nc, ident[:])
+        nc.scalar.dma_start(out=heat[:], in_=heater.rearrange("(g p t) -> p g t", g=2, t=4))
+        for g in range(2):
+            load_w(0, g)
+            load_q(g)
+        for g in range(2):
+            load_w(1, g)
+        for j in range(2, B // PAIR):
+            load_q(j)
+        nc.sync.dma_start(out=inv16[:], in_=inv_cap.rearrange("(g p t) -> p g t", g=2, t=4))
 
-        def store_some(c, h, blocks, engines="SSSS"):
-            for b, e in zip(blocks, engines):
-                store(c, h, b, e, nc.scalar if (c, h, e) == (LAST, 1, "S") else nc.sync)
+        group_w(0, 0, nc.vector.tensor_copy, 0, 2)
+        group_w(0, 0, nc.scalar.copy, 2, 4)
+        for b in range(2):
+            turn_q(0, b)
+            copy_q(0, b)
+        quantize_w(0, 0, 0, 4)
+        group_w(0, 1, nc.vector.tensor_copy, 0, 4)
+        group_w(1, 0, nc.scalar.copy, 2, 4)
+        for b in range(2):
+            turn_q(1, b)
+        for b in range(2):
+            copy_q(1, b)
+        quantize_q(0)
+        quantize_w(0, 1, 0, 4)
+        group_w(1, 1, nc.scalar.copy, 2, 4)
+        for g in range(2):
+            group_w(1, g, nc.vector.tensor_copy, 0, 2)
+        for g in range(2):
+            quantize_w(1, g, 0, 2)
+        nc.gpsimd.tensor_copy(out=inv[:], in_=inv16[:])
 
-        def widen():
-            nc.gpsimd.tensor_copy(out=inv[:], in_=inv16[:])
-
-        do = {"gw": group_w, "qw": quantize_w, "tq": turn_q, "cq": copy_q, "tp": turn_q_pair, "qq": quantize_q, "gs": group_state,
-              "qs": quantize_state, "fin": finish, "sc": scale, "wid": widen, "sort": sort_q, "warm": warm, "T": turn_pair, "C": copy_pair, "F": turn_out, "O": store_some}
-        for x in HEAD:
-            do[x[0]](*x[1:])
         units = [(s, c, h) for s, c in ORDER for h in range(2)]
-        made = {(0, 0, 0), (0, 0, 1)}
-        w_made = {x[1:] for x in HEAD if x[0] == "qw"}
-        ready = set()
+        ends = [sum(4 * WIDTH[u[1]] for u in units[: i + 1]) for i in range(len(units))]
+        closing = len(units) - 2
+        split = {0: 4, closing: LEAD - 2}
+        first_wide = units.index((0, 1, 0))
+        helped = [i for i, (s, c, h) in enumerate(units) if s < 2 and h == 0 and WIDTH[c] == WIDE and i != first_wide]
 
-        def may(x):
-            if x[0] == "M":
-                kind, i, t, gs = x
-                s, c, h = units[i]
-                return all((s, c, g) in made and any(y[:2] == (h, g) and (len(y) == 2 or y[2] <= t < y[3]) for y in w_made) for g in gs) and (0 not in gs or i in PACKED and t % 2 or len(free) > 0 and (gs == (0,) or len([k for k in number if k[0] == "m"]) < LEAD))
-            if x[0] == "tp":
-                return len(free) >= 2 and (FIRST[x[1]] + x[2] in sorted_q or FIRST[x[1]] + x[2] < 4)
-            return len(free) >= len(x[3]) and (x[1], x[2], 3) in ready or x[-1] is True and (x[1], x[2], 3) in ready
-
-        tensor = []
-        for i in range(len(units)):
-            if i in SPLIT:
-                tensor.extend([("M", i, t, (0,)) for t in range(4)])
-                tensor.extend(AFTER_M.get((i, -1), []))
+        tensor, pairs, results, since = [], [(c, j) for c, n in enumerate(WIDTH) for j in range(n // PAIR)][2:], [], 0
+        for i, (s, c, h) in enumerate(units):
+            if i == closing:
+                tensor += [("out", i - 1, *x[1:]) for x in results]
+                results = []
+            if i in split:
+                tensor += [("pass", i, t, (0,)) for t in range(split[i])]
             for t in range(4):
-                tensor.append(("M", i, t, (1,) if i in SPLIT else (0, 1)))
-                tensor.extend(AFTER_M.get((i, t), []))
+                tensor.append(("pass", i, t, (1,) if t < split.get(i, 0) else (0, 1)))
+                since += WIDTH[c]
+            if results and i < closing and since >= SPACING and ends[i] >= results[0][0] + UNIT:
+                tensor.append(("out", i, *results.pop(0)[1:]))
+                since = 0
+            if pairs and (i == 0 or h == 1):
+                tensor.append(("q", i, *pairs.pop(0)))
+            if s == 2:
+                results += [(ends[i], c, h, j) for j in range(WIDTH[c] // PAIR)]
+        tensor += [("out", i, *x[1:]) for x in results]
 
-        late = []
-        both = {}
+        made = {(0, 0, 0), (0, 0, 1)}
+        w_upper = [(1, 0), (1, 1)]
+        finished, late, ripening, both = set(), [], [], {}
 
-        def flush(n):
-            for y in list(late):
-                y[0] = y[0] - n
-                if y[0] <= 0:
-                    late.remove(y)
-                    do[y[1][0]](*y[1][1:])
+        def may(waiting, kind, *x):
+            if kind == "pass":
+                i, t, gs = x
+                s, c, h = units[i]
+                second = WIDTH[c] == PAIR and i not in split and t % 2
+                return all((s, c, g) in made for g in gs) and not (h and t > 1 and w_upper) and (0 not in gs or second or free)
+            if x[0] >= closing - 1 and not waiting:
+                return False
+            return (len(spare) >= 2 or waiting and len(free) == LEAD) and (kind == "q" or x[1:3] in finished)
 
-        def feed():
-            while tensor and may(tensor[0]):
-                x = tensor.pop(0)
-                if x[0] == "M":
-                    kind, i, t, gs = x
+        def feed(waiting=False):
+            while tensor and may(waiting, *tensor[0]):
+                kind, *x = tensor.pop(0)
+                if kind == "q":
+                    for b in range(2):
+                        turn_q(x[1], 2 * x[2] + b)
+                    late.append((kind, *x))
+                elif kind == "out":
+                    turn_out(*x[1:], waiting and len(free) == LEAD)
+                    late.append((kind, *x))
+                else:
+                    i, t, gs = x
                     s, c, h = units[i]
-                    packed = i in PACKED
-                    if packed and t % 2:
-                        held[(i, t)] = both[i][:, 1, :]
-                    elif packed:
-                        both[i] = take(("m", i, t + 1), [P, 2, PAIR])
-                        held[(i, t)] = both[i][:, 0, :]
+                    if WIDTH[c] == PAIR and i not in split:
+                        if t % 2 == 0:
+                            both[i] = take(("pass", i, t + 1), [P, 2, PAIR])
+                        held[(i, t)] = both[i][:, t % 2, :]
                     elif 0 in gs:
-                        bank = take(("m", i, t), [P, WIDTH[c]])
+                        bank = take(("pass", i, t), [P, WIDTH[c]])
                         held[(i, t)] = bank[:]
                     for g in gs:
                         one_pass(held[(i, t)], s, c, h, t, g)
-                elif x[0] == "tp":
-                    turn_pair(*x[1:])
-                    late.append([DELAY, ("C",) + x[1:]])
-                else:
-                    turn_out(x[1], x[2], x[3], x[-1] is True)
-                    if x[0] == "fin":
-                        late.append([DELAY, ("O",) + x[1:5]])
+
+        def empty(i):
+            while late and late[0][1] <= i:
+                kind, behind, *x = late.pop(0)
+                if kind == "out":
+                    store(*x, behind > closing)
+                    continue
+                for b in range(2):
+                    copy_q(x[0], 2 * x[1] + b)
+                if 2 * x[1] + 2 == WIDTH[x[0]] // P:
+                    ripening.append((ends[max(units.index((0, x[0], 0)) - 5, 0)], "q", x[0]))
+
+        def quantize(x):
+            ripening.remove(x)
+            if x[1] == "q":
+                quantize_q(x[2])
+                made.update([(0, x[2], 0), (0, x[2], 1)])
+            else:
+                quantize_state(*x[1:])
+                made.add((x[1] + 1, x[2], x[3]))
+            feed()
 
         for i, (s, c, h) in enumerate(units):
             for t in range(4):
                 feed()
-                advance(held.pop((i, t)), s, c, h, t)
-                if ("m", i, t) in number:
-                    give(("m", i, t))
-                if s == 2:
-                    ready.add((c, h, t))
-                flush(1)
-                if i == len(units) - 1:
-                    feed()
-                for x in AFTER_A.get((i, t), []):
-                    if x[0] == "qq":
-                        flush(9)
-                    do[x[0]](*x[1:])
-                    if x[0] == "qs":
-                        made.add((x[1] + 1, x[2], x[3]))
-                    if x[0] == "qq":
-                        made.add((0, x[1], 0))
-                        made.add((0, x[1], 1))
-                    if x[0] == "qw":
-                        w_made.add(x[1:])
-                    feed()
-        while tensor or late:
-            feed()
-            flush(9)
+                if t or i not in helped:
+                    add_on_vector(held.pop((i, t)), s, c, h, t)
+                if ("pass", i, t) in number:
+                    give(("pass", i, t))
+                if i == 0 and t % 2:
+                    quantize_w(*w_upper.pop(0), 2, 4)
+                if s == 2 and c < LAST and t < ON_GPSIMD:
+                    scale(nc.gpsimd, state[c][h], c, h, t)
+                elif s == 2 and c < LAST:
+                    nc.scalar.mul(state[c][h][:, t, :], state[c][h][:, t, :], inv[:, h, t : t + 1])
+                if (s, c, h) == (1, LAST, 0):
+                    scale(nc.gpsimd, scaled[0], c, h, t)
+                if h == 1 and t == 3 - AHEAD and i + 1 < closing:
+                    s1, c1 = units[i + 1][:2]
+                    for x in [x for x in ripening if x[1:3] == (("q", c1) if s1 == 0 else (s1 - 1, c1))]:
+                        quantize(x)
+            if i + 1 == closing:
+                feed(waiting=True)
+                group_state(s, c, h, nc.vector.tensor_copy)
+                ripening.append((ends[i], s, c, h))
+            for x in [x for x in ripening if x[0] <= ends[i] and (h == 1 or x[1] != "q")]:
+                quantize(x)
+            if i == 0:
+                empty(i)
+            if i + 1 in helped:
+                feed()
+                add_on_others(held.pop((i + 1, 0)), *units[i + 1], 0)
+            if s == 2:
+                finished.add((c, h))
+            elif i + 1 < closing:
+                group_state(s, c, h, nc.scalar.copy)
+                ripening.append((ends[i] + 4 * WIDTH[c], s, c, h))
+            else:
+                for t in range(4):
+                    scale(nc.vector, scaled[1], c, h, t)
+            while i + 1 == closing and tensor[0][0] == "out":
+                empty(i)
+                feed(waiting=True)
+            empty(i)
+        while tensor:
+            feed(waiting=True)
+            empty(i)

@@ -49,16 +49,15 @@ def tile_dense_heat_steps_t1_kernel(tc, q, w, heater, inv_cap, out):
         scaled = [keep.tile([P, 4, WIDTH[LAST]], F32, name="scaled%d" % h) for h in range(2)]
 
         q_rows, w_rows, w_grouped, grouped, codes, turned, held = {}, {}, {}, {}, {}, {}, {}
-        free, spare, number = list(range(LEAD)), list(range(LEAD, 8)), {}
+        free, number = list(range(8)), {}
 
-        def take(key, shape, lent=False):
-            number[key] = free.pop(0) if key[0] == "pass" or lent else spare.pop(0)
+        def take(key, shape):
+            number[key] = free.pop(0)
             bank = psum.tile(shape, F32, name="bank%d" % number[key])
             return bank
 
         def give(key):
-            n = number.pop(key)
-            (free if n < LEAD else spare).append(n)
+            free.append(number.pop(key))
 
         def hbm_rows(x, j):
             return x[PAIR * j : PAIR * (j + 1), :].rearrange("(p b) k -> p b k", b=2)
@@ -164,10 +163,10 @@ def tile_dense_heat_steps_t1_kernel(tc, q, w, heater, inv_cap, out):
             src = grouped[(s, c, h)][:].rearrange("p n t -> p (n t)")
             nc.vector.quantize_mx(out=cd[:, h, :].bitcast(FP8X4), scales=sc[:, h, :], in_=src)
 
-        def turn_out(c, h, pair, lent):
+        def turn_out(c, h, pair):
             blocks = (2 * pair, 2 * pair + 1)
             for b in blocks:
-                turned[(c, h, b)] = take((c, h, b), [P, 4, P], lent)
+                turned[(c, h, b)] = take((c, h, b), [P, 4, P])
             by_block = [(b, t) for b in blocks for t in range(4)]
             by_tile = [(b, t) for t in range(4) for b in blocks]
             for b, t in by_tile if (c, h) == (LAST, 1) else by_block:
@@ -217,9 +216,10 @@ def tile_dense_heat_steps_t1_kernel(tc, q, w, heater, inv_cap, out):
         units = [(s, c, h) for s, c in ORDER for h in range(2)]
         ends = [sum(4 * WIDTH[u[1]] for u in units[: i + 1]) for i in range(len(units))]
         closing = len(units) - 2
-        split = {0: 4, closing: LEAD - 2}
+        split = {0: 4, closing: 2}
         first_wide = units.index((0, 1, 0))
-        helped = [i for i, (s, c, h) in enumerate(units) if s < 2 and h == 0 and WIDTH[c] == WIDE and i != first_wide]
+        crowded = units.index((2, 1, 0))
+        helped = [i for i, (s, c, h) in enumerate(units) if s < 2 and h == 0 and WIDTH[c] == WIDE and first_wide < i < crowded]
 
         tensor, pairs, results, since = [], [(c, j) for c, n in enumerate(WIDTH) for j in range(n // PAIR)][2:], [], 0
         for i, (s, c, h) in enumerate(units):
@@ -249,10 +249,10 @@ def tile_dense_heat_steps_t1_kernel(tc, q, w, heater, inv_cap, out):
                 i, t, gs = x
                 s, c, h = units[i]
                 second = WIDTH[c] == PAIR and i not in split and t % 2
-                return all((s, c, g) in made for g in gs) and not (h and t > 1 and w_upper) and (0 not in gs or second or free)
+                return all((s, c, g) in made for g in gs) and not (h and t > 1 and w_upper) and (0 not in gs or second or free and len([k for k in number if k[0] == "pass"]) < LEAD)
             if x[0] >= closing - 1 and not waiting:
                 return False
-            return (len(spare) >= 2 or waiting and len(free) == LEAD) and (kind == "q" or x[1:3] in finished)
+            return len(free) >= 2 and (kind == "q" or x[1:3] in finished)
 
         def feed(waiting=False):
             while tensor and may(waiting, *tensor[0]):
@@ -262,7 +262,7 @@ def tile_dense_heat_steps_t1_kernel(tc, q, w, heater, inv_cap, out):
                         turn_q(x[1], 2 * x[2] + b)
                     late.append((kind, *x))
                 elif kind == "out":
-                    turn_out(*x[1:], waiting and len(free) == LEAD)
+                    turn_out(*x[1:])
                     late.append((kind, *x))
                 else:
                     i, t, gs = x
@@ -299,15 +299,18 @@ def tile_dense_heat_steps_t1_kernel(tc, q, w, heater, inv_cap, out):
             feed()
 
         for i, (s, c, h) in enumerate(units):
+            copying = units[i - 1][0] < 2 and WIDTH[units[i - 1][1]] == WIDE
             for t in range(4):
                 feed()
                 if t or i not in helped:
                     add_on_vector(held.pop((i, t)), s, c, h, t)
                 if ("pass", i, t) in number:
                     give(("pass", i, t))
+                if t == 2:
+                    empty(i)
                 if i == 0 and t % 2:
                     quantize_w(*w_upper.pop(0), 2, 4)
-                if s == 2 and c < LAST and t < ON_GPSIMD:
+                if s == 2 and c < LAST and t < ON_GPSIMD and not copying:
                     scale(nc.gpsimd, state[c][h], c, h, t)
                 elif s == 2 and c < LAST:
                     nc.scalar.mul(state[c][h][:, t, :], state[c][h][:, t, :], inv[:, h, t : t + 1])

@@ -147,10 +147,10 @@ def tile_dense_heat_steps_t1_kernel(tc, q, w, heater, inv_cap, out):
         def scale(engine, dst, c, h, t):
             engine.tensor_scalar(dst[:, t, :], state[c][h][:, t, :], inv[:, h, t : t + 1], 0.0, MULT, ADD)
 
-        def group_state(s, c, h, copy):
+        def group_state(s, c, h, copy, share):
             dst = stage.tile([P, WIDTH[c], 4], BF16, name="half", align_bytes=256)
             grouped[(s, c, h)] = dst
-            n = min(SHARE, WIDTH[c])
+            n = min(share, WIDTH[c])
             copy(
                 out=dst[:, :n, :].rearrange("p (c i) t -> p c t i", i=4),
                 in_=state[c][h][:, :, :n].rearrange("p t (c i) -> p c t i", i=4),
@@ -220,6 +220,7 @@ def tile_dense_heat_steps_t1_kernel(tc, q, w, heater, inv_cap, out):
         first_wide = units.index((0, 1, 0))
         crowded = units.index((2, 1, 0))
         helped = [i for i, (s, c, h) in enumerate(units) if s < 2 and h == 0 and WIDTH[c] == WIDE and first_wide < i < crowded]
+        helped += [i + 1 for i in helped if units.index((units[i][0] + 1, units[i][1], 0)) - i > 4]
 
         tensor, pairs, results, since = [], [(c, j) for c, n in enumerate(WIDTH) for j in range(n // PAIR)][2:], [], 0
         for i, (s, c, h) in enumerate(units):
@@ -322,7 +323,7 @@ def tile_dense_heat_steps_t1_kernel(tc, q, w, heater, inv_cap, out):
                         quantize(x)
             if i + 1 == closing:
                 feed(waiting=True)
-                group_state(s, c, h, nc.vector.tensor_copy)
+                group_state(s, c, h, nc.vector.tensor_copy, SHARE)
                 ripening.append((ends[i], s, c, h))
             for x in [x for x in ripening if x[0] <= ends[i] and (h == 1 or x[1] != "q")]:
                 quantize(x)
@@ -334,8 +335,9 @@ def tile_dense_heat_steps_t1_kernel(tc, q, w, heater, inv_cap, out):
             if s == 2:
                 finished.add((c, h))
             elif i + 1 < closing:
-                group_state(s, c, h, nc.scalar.copy)
-                ripening.append((ends[i] + 4 * WIDTH[c], s, c, h))
+                alone = h == 0 and i + 1 in helped
+                group_state(s, c, h, nc.scalar.copy, WIDE if alone else SHARE)
+                ripening.append((ends[i] + 4 * WIDTH[c] * (1 + alone), s, c, h))
             else:
                 for t in range(4):
                     scale(nc.vector, scaled[1], c, h, t)

from contextlib import ExitStack

import concourse.mybir as mybir
from concourse.masks import make_identity

B, N = 1536, 1024
FLOPS = 3 * 2 * B * N * N

F32 = mybir.dt.float32
BF16 = mybir.dt.bfloat16
U32 = mybir.dt.uint32
U8 = mybir.dt.uint8
FP8X4 = mybir.dt.float8_e4m3fn_x4
ADD = mybir.AluOpType.add
MULT = mybir.AluOpType.mult
IDENTITY = mybir.ActivationFunctionType.Identity

P = 128
PAIR = 2 * P
WIDE = 512
UNIT = 4 * WIDE
WIDTH = [PAIR, WIDE, WIDE, PAIR]
FIRST = [sum(WIDTH[:c]) // PAIR for c in range(len(WIDTH))]
LAST = len(WIDTH) - 1
ORDER = [(0, 0), (0, 1), (1, 0), (1, 1), (2, 0), (0, 2), (2, 1), (1, 2), (0, 3), (2, 2), (1, 3), (2, 3)]
LEAD = 4
AHEAD = 2
SPACING = 2048
SHARE = 256
ON_GPSIMD = 2


def tile_dense_heat_steps_t1_kernel(tc, q, w, heater, inv_cap, out):
    nc = tc.nc
    with ExitStack() as ctx:
        keep = ctx.enter_context(tc.tile_pool(name="keep", bufs=1))
        stage = ctx.enter_context(tc.tile_pool(name="stage", bufs=8))
        psum = ctx.enter_context(tc.psum_pool(name="psum", bufs=1))
        ctx.enter_context(tc.manual_schedule())

        ident = keep.tile([P, P], F32, name="ident")
        heat = keep.tile([P, 2, 4], BF16, name="heat")
        inv16 = keep.tile([P, 2, 4], BF16, name="inv16")
        inv = keep.tile([P, 2, 4], F32, name="inv")
        w_codes = keep.tile([P, 2, 2, 512], U32, name="w_codes", align_bytes=256)
        w_scales = keep.tile([P, 2, 2, 512], U8, name="w_scales", align_bytes=256)
        q_words = [keep.tile([P, 2, n, 4], BF16, name="q_words%d" % c, align_bytes=256) for c, n in enumerate(WIDTH)]
        state = [[keep.tile([P, 4, n], F32, name="state%d%d" % (c, h)) for h in range(2)] for c, n in enumerate(WIDTH)]
        scaled = [keep.tile([P, 4, WIDTH[LAST]], F32, name="scaled%d" % h) for h in range(2)]

        q_rows, w_rows, w_grouped, grouped, codes, turned, held = {}, {}, {}, {}, {}, {}, {}
        free, number = list(range(8)), {}

        def take(key, shape):
            number[key] = free.pop(0)
            bank = psum.tile(shape, F32, name="bank%d" % number[key])
            return bank

        def give(key):
            free.append(number.pop(key))

        def hbm_rows(x, j):
            return x[PAIR * j : PAIR * (j + 1), :].rearrange("(p b) k -> p b k", b=2)

        def load_q(j):
            q_rows[j] = keep.tile([P, 2, N], BF16, name="q_rows%d" % j, align_bytes=256)
            nc.sync.dma_start(out=q_rows[j][:], in_=hbm_rows(q, j))

        def load_w(h, g):
            w_rows[(h, g)] = stage.tile([P, 4, 512], BF16, name="half", align_bytes=256)
            src = w[512 * g : 512 * (g + 1), 512 * h : 512 * (h + 1)].rearrange("(p j) c -> p j c", j=4)
            nc.sync.dma_start(out=w_rows[(h, g)][:], in_=src)

        def codes_of(s, c):
            if (s, c) not in codes:
                cd = keep.tile([P, 2, WIDTH[c]], U32, name="codes%d%d" % (s % 2, c), align_bytes=256)
                sc = keep.tile([P, 2, WIDTH[c]], U8, name="scales%d%d" % (s % 2, c), align_bytes=256)
                codes[(s, c)] = (cd, sc)
            return codes[(s, c)]

        def group_w(h, g, copy, t0, t1):
            if (h, g) not in w_grouped:
                w_grouped[(h, g)] = stage.tile([P, 2048], BF16, name="half", align_bytes=256)
            copy(
                out=w_grouped[(h, g)][:].rearrange("p (t m i j) -> p m t i j", t=4, i=2, j=4)[:, :, t0:t1],
                in_=w_rows[(h, g)][:].rearrange("p j (m i t) -> p m t i j", t=4, i=2)[:, :, t0:t1],
            )

        def quantize_w(h, g, t0, t1):
            nc.vector.quantize_mx(
                out=w_codes[:, h, g, P * t0 : P * t1].bitcast(FP8X4),
                scales=w_scales[:, h, g, P * t0 : P * t1],
                in_=w_grouped[(h, g)][:, 512 * t0 : 512 * t1],
            )

        def turn_q(c, b):
            words = q_rows[FIRST[c] + b // 2][:, b % 2, :].bitcast(F32)
            turned[("q", c, b)] = take(("q", c, b), [P, 4, P])
            for g in range(2):
                for u in range(2):
                    nc.tensor.transpose(turned[("q", c, b)][:, 2 * g + u, :], words[:, 256 * g + u : 256 * (g + 1) : 2], ident[:])

        def copy_q(c, b):
            dst = q_words[c][:, :, P * b : P * (b + 1), :].rearrange("p g n t -> p g (n t)").bitcast(F32)
            src = turned[("q", c, b)][:].rearrange("p (g u) n -> p g n u", g=2)
            nc.scalar.copy(out=dst.rearrange("p g (n u) -> p g n u", u=2), in_=src)
            give(("q", c, b))

        def quantize_q(c):
            cd, sc = codes_of(0, c)
            nc.vector.quantize_mx(
                out=cd[:].rearrange("p g n -> p (g n)").bitcast(FP8X4),
                scales=sc[:].rearrange("p g n -> p (g n)"),
                in_=q_words[c][:].rearrange("p g n t -> p (g n t)"),
            )

        def one_pass(bank, s, c, h, t, g):
            cd, sc = codes_of(s, c)
            cells = slice(P * t, P * (t + 1))
            nc.tensor.matmul_mx(
                out=bank,
                lhsT=w_codes[:, h, g, cells].bitcast(FP8X4),
                lhsT_scale=w_scales[:, h, g, cells],
                rhs=cd[:, g, :].bitcast(FP8X4),
                rhs_scale=sc[:, g, :],
                start=(g == 0),
                stop=(g == 1),
            )

        def add_on_vector(bank, s, c, h, t):
            now = state[c][h][:, t, :]
            if s == 0:
                nc.vector.scalar_tensor_tensor(now, bank, heat[:, h, t : t + 1], q_words[c][:, h, :, t], ADD, ADD)
            elif s == 1:
                nc.vector.scalar_tensor_tensor(now, bank, heat[:, h, t : t + 1], now, ADD, ADD)
            elif c == LAST:
                nc.vector.scalar_tensor_tensor(now, bank, inv[:, h, t : t + 1], scaled[h][:, t, :], MULT, ADD)
            else:
                nc.vector.tensor_tensor(now, bank, now, ADD)

        def add_on_others(bank, s, c, h, t):
            now = state[c][h][:, t, :]
            part = stage.tile([P, WIDE], F32, name="part", bufs=2)
            nc.scalar.activation(part[:], bank, IDENTITY, bias=heat[:, h, t : t + 1])
            nc.gpsimd.tensor_tensor(now, part[:], q_words[c][:, h, :, t] if s == 0 else now, ADD)

        def scale(engine, dst, c, h, t):
            engine.tensor_scalar(dst[:, t, :], state[c][h][:, t, :], inv[:, h, t : t + 1], 0.0, MULT, ADD)

        def group_state(s, c, h, copy, share):
            dst = stage.tile([P, WIDTH[c], 4], BF16, name="half", align_bytes=256)
            grouped[(s, c, h)] = dst
            n = min(share, WIDTH[c])
            copy(
                out=dst[:, :n, :].rearrange("p (c i) t -> p c t i", i=4),
                in_=state[c][h][:, :, :n].rearrange("p t (c i) -> p c t i", i=4),
            )
            if n < WIDTH[c]:
                nc.gpsimd.tensor_scalar(dst[:, n:, :], state[c][h][:, :, n:].rearrange("p t n -> p n t"), 1.0, 0.0, MULT, ADD)

        def quantize_state(s, c, h):
            cd, sc = codes_of(s + 1, c)
            src = grouped[(s, c, h)][:].rearrange("p n t -> p (n t)")
            nc.vector.quantize_mx(out=cd[:, h, :].bitcast(FP8X4), scales=sc[:, h, :], in_=src)

        def turn_out(c, h, pair):
            blocks = (2 * pair, 2 * pair + 1)
            for b in blocks:
                turned[(c, h, b)] = take((c, h, b), [P, 4, P])
            by_block = [(b, t) for b in blocks for t in range(4)]
            by_tile = [(b, t) for t in range(4) for b in blocks]
            for b, t in by_tile if (c, h) == (LAST, 1) else by_block:
                nc.tensor.transpose(turned[(c, h, b)][:, t, :], state[c][h][:, t, P * b : P * (b + 1)], ident[:])

        def store(c, h, pair, shared):
            for b in (2 * pair, 2 * pair + 1):
                copy = nc.vector.tensor_copy if shared and b % 2 else nc.scalar.copy
                queue = nc.scalar if (c, h, b) == (LAST, 1, 0) else nc.sync
                res = stage.tile([P, 512], F32, name="res")
                copy(out=res[:].rearrange("p (m t) -> p m t", t=4), in_=turned[(c, h, b)][:].rearrange("p t m -> p m t"))
                give((c, h, b))
                queue.dma_start(out=hbm_rows(out, FIRST[c] + pair)[:, b % 2, 512 * h : 512 * (h + 1)], in_=res[:])

        make_identity(nc, ident[:])
        nc.scalar.dma_start(out=heat[:], in_=heater.rearrange("(g p t) -> p g t", g=2, t=4))
        for g in range(2):
            load_w(0, g)
            load_q(g)
        for g in range(2):
            load_w(1, g)
        for j in range(2, B // PAIR):
            load_q(j)
        nc.sync.dma_start(out=inv16[:], in_=inv_cap.rearrange("(g p t) -> p g t", g=2, t=4))

        group_w(0, 0, nc.vector.tensor_copy, 0, 2)
        group_w(0, 0, nc.scalar.copy, 2, 4)
        for b in range(2):
            turn_q(0, b)
            copy_q(0, b)
        quantize_w(0, 0, 0, 4)
        group_w(0, 1, nc.vector.tensor_copy, 0, 4)
        group_w(1, 0, nc.scalar.copy, 2, 4)
        for b in range(2):
            turn_q(1, b)
        for b in range(2):
            copy_q(1, b)
        quantize_q(0)
        quantize_w(0, 1, 0, 4)
        group_w(1, 1, nc.scalar.copy, 2, 4)
        for g in range(2):
            group_w(1, g, nc.vector.tensor_copy, 0, 2)
        for g in range(2):
            quantize_w(1, g, 0, 2)
        nc.gpsimd.tensor_copy(out=inv[:], in_=inv16[:])

        units = [(s, c, h) for s, c in ORDER for h in range(2)]
        ends = [sum(4 * WIDTH[u[1]] for u in units[: i + 1]) for i in range(len(units))]
        closing = len(units) - 2
        split = {0: 4, closing: 2}
        first_wide = units.index((0, 1, 0))
        crowded = units.index((2, 1, 0))
        helped = [i for i, (s, c, h) in enumerate(units) if s < 2 and h == 0 and WIDTH[c] == WIDE and first_wide < i < crowded]
        helped += [i + 1 for i in helped if units.index((units[i][0] + 1, units[i][1], 0)) - i > 4]

        tensor, pairs, results, since = [], [(c, j) for c, n in enumerate(WIDTH) for j in range(n // PAIR)][2:], [], 0
        for i, (s, c, h) in enumerate(units):
            if i == closing:
                tensor += [("out", i - 1, *x[1:]) for x in results]
                results = []
            if i in split:
                tensor += [("pass", i, t, (0,)) for t in range(split[i])]
            for t in range(4):
                tensor.append(("pass", i, t, (1,) if t < split.get(i, 0) else (0, 1)))
                since += WIDTH[c]
            if results and i < closing and since >= SPACING and ends[i] >= results[0][0] + UNIT:
                tensor.append(("out", i, *results.pop(0)[1:]))
                since = 0
            if pairs and (i == 0 or h == 1):
                tensor.append(("q", i, *pairs.pop(0)))
            if s == 2:
                results += [(ends[i], c, h, j) for j in range(WIDTH[c] // PAIR)]
        tensor += [("out", i, *x[1:]) for x in results]

        made = {(0, 0, 0), (0, 0, 1)}
        w_upper = [(1, 0), (1, 1)]
        finished, late, ripening, both = set(), [], [], {}

        def may(waiting, kind, *x):
            if kind == "pass":
                i, t, gs = x
                s, c, h = units[i]
                second = WIDTH[c] == PAIR and i not in split and t % 2
                return all((s, c, g) in made for g in gs) and not (h and t > 1 and w_upper) and (0 not in gs or second or free and len([k for k in number if k[0] == "pass"]) < LEAD)
            if x[0] >= closing - 1 and not waiting:
                return False
            return len(free) >= 2 and (kind == "q" or x[1:3] in finished)

        def feed(waiting=False):
            while tensor and may(waiting, *tensor[0]):
                kind, *x = tensor.pop(0)
                if kind == "q":
                    for b in range(2):
                        turn_q(x[1], 2 * x[2] + b)
                    late.append((kind, *x))
                elif kind == "out":
                    turn_out(*x[1:])
                    late.append((kind, *x))
                else:
                    i, t, gs = x
                    s, c, h = units[i]
                    if WIDTH[c] == PAIR and i not in split:
                        if t % 2 == 0:
                            both[i] = take(("pass", i, t + 1), [P, 2, PAIR])
                        held[(i, t)] = both[i][:, t % 2, :]
                    elif 0 in gs:
                        bank = take(("pass", i, t), [P, WIDTH[c]])
                        held[(i, t)] = bank[:]
                    for g in gs:
                        one_pass(held[(i, t)], s, c, h, t, g)

        def empty(i):
            while late and late[0][1] <= i:
                kind, behind, *x = late.pop(0)
                if kind == "out":
                    store(*x, behind > closing)
                    continue
                for b in range(2):
                    copy_q(x[0], 2 * x[1] + b)
                if 2 * x[1] + 2 == WIDTH[x[0]] // P:
                    ripening.append((ends[max(units.index((0, x[0], 0)) - 5, 0)], "q", x[0]))

        def quantize(x):
            ripening.remove(x)
            if x[1] == "q":
                quantize_q(x[2])
                made.update([(0, x[2], 0), (0, x[2], 1)])
            else:
                quantize_state(*x[1:])
                made.add((x[1] + 1, x[2], x[3]))
            feed()

        for i, (s, c, h) in enumerate(units):
            copying = units[i - 1][0] < 2 and WIDTH[units[i - 1][1]] == WIDE
            for t in range(4):
                feed()
                if t or i not in helped:
                    add_on_vector(held.pop((i, t)), s, c, h, t)
                if ("pass", i, t) in number:
                    give(("pass", i, t))
                if t == 2:
                    empty(i)
                if i == 0 and t % 2:
                    quantize_w(*w_upper.pop(0), 2, 4)
                if s == 2 and c < LAST and t < ON_GPSIMD and not copying:
                    scale(nc.gpsimd, state[c][h], c, h, t)
                elif s == 2 and c < LAST:
                    nc.scalar.mul(state[c][h][:, t, :], state[c][h][:, t, :], inv[:, h, t : t + 1])
                if (s, c, h) == (1, LAST, 0):
                    scale(nc.gpsimd, scaled[0], c, h, t)
                if h == 1 and t == 3 - AHEAD and i + 1 < closing:
                    s1, c1 = units[i + 1][:2]
                    for x in [x for x in ripening if x[1:3] == (("q", c1) if s1 == 0 else (s1 - 1, c1))]:
                        quantize(x)
            if i + 1 == closing:
                feed(waiting=True)
                group_state(s, c, h, nc.vector.tensor_copy, SHARE)
                ripening.append((ends[i], s, c, h))
            for x in [x for x in ripening if x[0] <= ends[i] and (h == 1 or x[1] != "q")]:
                quantize(x)
            if i == 0:
                empty(i)
            if i + 1 in helped:
                feed()
                add_on_others(held.pop((i + 1, 0)), *units[i + 1], 0)
            if s == 2:
                finished.add((c, h))
            elif i + 1 < closing:
                alone = h == 0 and i + 1 in helped
                group_state(s, c, h, nc.scalar.copy, WIDE if alone else SHARE)
                ripening.append((ends[i] + 4 * WIDTH[c] * (1 + alone), s, c, h))
            else:
                for t in range(4):
                    scale(nc.vector, scaled[1], c, h, t)
            while i + 1 == closing and tensor[0][0] == "out":
                empty(i)
                feed(waiting=True)
            empty(i)
        while tensor:
            feed(waiting=True)
            empty(i)
